import numpy as np
import ml_dtypes


def mxq(x, axis, fmt="e4m3"):
    dtype, down = {"e4m3": (ml_dtypes.float8_e4m3fn, 7), "e5m2": (ml_dtypes.float8_e5m2, 14)}[fmt]
    v = np.moveaxis(np.asarray(x, np.float32).astype(ml_dtypes.bfloat16).astype(np.float64), axis, -1)
    blocks = v.reshape(v.shape[:-1] + (-1, 32))
    amax = np.abs(blocks).max(-1, keepdims=True)
    byte = np.maximum(np.where(amax > 0, np.frexp(amax)[1] - 1 + 127, 0) - down, 1)
    scale = np.exp2(byte - 127.0)
    codes = (blocks / scale).astype(np.float32).astype(dtype).astype(np.float64)
    return np.moveaxis((codes * scale).reshape(v.shape), -1, axis)


WIDE = False


def mx_kscale(k):
    if not WIDE:
        return np.ones(k)
    levels = np.array([18, -18])
    if k % 512:
        return np.exp2(np.random.permutation(np.resize(levels, k // 32))).repeat(32)
    a = np.empty((k // 512, 16))
    for p in range(k // 512):
        a[p, :8] = np.random.permutation(np.resize(levels, 8))
        for g in range(8):
            far = levels[np.abs(levels - a[p, g]) >= 10]
            a[p, g + 8] = far[np.random.randint(len(far))]
    return np.exp2(a.ravel()).repeat(32)


def f64(x):
    return np.asarray(x).astype(np.float64)


def striped(idx):
    return np.tile(np.asarray(idx).reshape(-1, 16).T, (8, 1)).astype(np.uint16)


def unstriped(offs):
    return offs[:16].T.reshape(-1).astype(np.int64)


B, N, T, D, R = 1, 512, 2048, 512, 1024


def setup_inputs():
    n = np.random.standard_normal
    idx = np.random.permutation(T)[:B * N]
    s = mx_kscale(D)[:, None]
    z = mx_kscale(R)[:, None]
    u = np.ones(T)
    u[idx] = mx_kscale(B * N)
    r = np.random.uniform(0.5, 2.0, T) * u
    x = n((B, D, R))
    return {
        "xT": (x * s).astype(np.float32),
        "wT": (n((D, T)) * (1.00 / np.sqrt(D)) / s / r).astype(np.float32),
        "y": (2 * np.random.randint(0, 2, (B, R, N)) - 1).astype(np.float32),
        "wt": (np.random.uniform(0.5, 1.5, (B, R, 1)) * 1.0 / np.sqrt(R) * z).astype(np.float32),
        "ts": np.tile(r, (128, 1)).astype(np.float32),
        "xm": (x.transpose(0, 2, 1) / z).astype(np.float32),
        "offs": striped(idx),
    }


def reference(xT, wT, y, wt, ts, xm, offs):
    idx = unstriped(offs)
    pick = lambda x: x[:, idx].reshape(x.shape[0], B, N).transpose(1, 0, 2)
    w = pick(f64(wT))
    a = mxq(f64(xT), 1, "e4m3").transpose(0, 2, 1) @ mxq(w, 1, "e4m3")
    ts_ = pick(f64(ts))[:, :1, :]
    a = a * ts_
    g = -f64(wt) * f64(y) / (1.0 + np.exp(f64(y) * a))
    g = g * ts_
    dw = mxq(f64(xm), 1, "e4m3").transpose(0, 2, 1) @ mxq(g, 1, "e5m2")
    gw = np.zeros((D, T))
    gw[:, idx] = dw.transpose(1, 0, 2).reshape(D, B * N)
    gx = mxq(g, 2, "e5m2") @ mxq(w, 2, "e4m3").transpose(0, 2, 1)
    return gw, gx

@@ -1,0 +1,236 @@
+from contextlib import ExitStack
+
+import concourse.mybir as mybir
+from concourse.masks import make_identity
+
+N, T, D, R = 512, 2048, 512, 1024
+FLOPS = 3 * 2 * N * D * R
+BYTES = 4 * (2 * D * R + 2 * D * T + R * N + R + T + R * D) + 2 * 128 * (N // 16)
+
+F32 = mybir.dt.float32
+BF16 = mybir.dt.bfloat16
+U32 = mybir.dt.uint32
+U16 = mybir.dt.uint16
+U8 = mybir.dt.uint8
+E4M3 = mybir.dt.float8_e4m3fn_x4
+E5M2 = mybir.dt.float8_e5m2_x4
+ALU = mybir.AluOpType
+ACT = mybir.ActivationFunctionType
+
+P = 128
+PACK = 4
+K_PASS = P * PACK
+ROW_PASSES = R // K_PASS
+
+
+def tile_attend_gsig_wx_ts_kernel(tc, xT, wT, y, wt, ts, xm, offs, out_0, out_1):
+    nc = tc.nc
+    with ExitStack() as ctx:
+        keep = ctx.enter_context(tc.tile_pool(name="keep", bufs=1))
+        raw = ctx.enter_context(tc.tile_pool(name="raw", bufs=3))
+        psum = ctx.enter_context(tc.psum_pool(name="psum", bufs=1))
+
+        def quantise(name, grouped, fmt):
+            codes = keep.tile([P, K_PASS], U32, name=name + "_codes", align_bytes=64)
+            scales = keep.tile([P, K_PASS], U8, name=name + "_scales", align_bytes=64)
+            nc.vector.quantize_mx(out=codes[:].bitcast(fmt), scales=scales[:], in_=grouped)
+            return codes, scales, fmt
+
+        def multiply(bank, stationary, q, moving, start, stop):
+            cols = slice(q * P, (q + 1) * P)
+            nc.tensor.matmul_mx(
+                out=bank[:],
+                lhsT=stationary[0][:, cols].bitcast(stationary[2]),
+                lhsT_scale=stationary[1][:, cols],
+                rhs=moving[0][:].bitcast(moving[2]),
+                rhs_scale=moving[1][:],
+                start=start,
+                stop=stop,
+            )
+
+        def turn(grouped, u):
+            words = grouped[:].bitcast(F32)
+            bank = psum.tile([P, PACK, P], F32, name="turn_bank", bufs=3)
+            for place in range(PACK):
+                nc.tensor.transpose(bank[:, place, :], words[:, 2 * place + u : 2 * N : 2 * PACK], identity[:])
+            return bank[:].rearrange("s a p -> s (a p)").bitcast(BF16).rearrange("s (a p e) -> s a p e", a=PACK, e=2)
+
+        offsets = keep.tile([P, N // 16], U16, name="offsets")
+        nc.sync.dma_start(offsets[:], offs)
+        ts_cols = keep.tile([P, T // P], F32, name="ts_cols")
+        nc.sync.dma_start(ts_cols[:], ts[0, :].rearrange("(n k) -> n k", k=T // P))
+        w_planes = []
+        for j in range(PACK):
+            plane = keep.tile([P, T], F32, name="w_plane%d" % j)
+            nc.sync.dma_start(plane[:], wT.rearrange("(p j) c -> p j c", j=PACK)[:, j, :])
+            w_planes.append(plane)
+        weights = keep.tile([P, ROW_PASSES, PACK], F32, name="weights")
+        nc.sync.dma_start(weights[:], wt[0].rearrange("(g p t) o -> p g (t o)", p=P, t=PACK))
+        x_view = xT[0].rearrange("(p j) r -> p j r", j=PACK)
+        y_view = y[0].rearrange("(g p t) i -> g p t i", p=P, t=PACK)
+        xm_view = xm[0].rearrange("(g p t) d -> g p t d", p=P, t=PACK)
+        x_raw = []
+        signed = []
+        for g in range(ROW_PASSES):
+            halves = []
+            for half in range(2):
+                piece = keep.tile([P, PACK, K_PASS // 2], F32, name="x_raw%d%d" % (g, half))
+                c0 = g * K_PASS + half * (K_PASS // 2)
+                nc.sync.dma_start(piece[:], x_view[:, :, c0 : c0 + K_PASS // 2])
+                halves.append(piece)
+            x_raw.append(halves)
+            labels = keep.tile([P, PACK, N], F32, name="signed%d" % g)
+            for half in range(2):
+                nc.sync.dma_start(labels[:, 2 * half : 2 * half + 2, :], y_view[g][:, 2 * half : 2 * half + 2, :])
+            signed.append(labels)
+        xm_raw = []
+        for g in range(ROW_PASSES):
+            rows = raw.tile([P, PACK, D], F32, name="rows")
+            nc.sync.dma_start(rows[:], xm_view[g])
+            xm_raw.append(rows)
+
+        identity = keep.tile([P, P], F32, name="identity")
+        make_identity(nc, identity[:])
+        warm = keep.tile([P, 1], F32, name="warm")
+        nc.scalar.activation(warm[:], identity[:, 0:1], ACT.Sigmoid)
+        windows = []
+        for j in range(D // P):
+            window = keep.tile([P, T], F32, name="window%d" % j)
+            nc.vector.memset(window[:], 0.0)
+            windows.append(window)
+
+        ts_all = keep.tile([P, T], F32, name="ts_all")
+        per = T // P
+        for b in range(per // PACK):
+            bank = psum.tile([P, PACK, P], F32, name="turn_bank", bufs=3)
+            for kk in range(PACK):
+                k = PACK * b + kk
+                nc.tensor.transpose(bank[:, kk, :], ts_cols[:, k : k + 1].to_broadcast([P, P]), identity[:])
+            nc.scalar.copy(
+                ts_all[:].rearrange("p (n k) -> p n k", k=per)[:, :, PACK * b : PACK * (b + 1)],
+                bank[:].rearrange("p k n -> p n k"),
+            )
+
+        w_by_d = keep.tile([P, N * PACK], BF16, name="w_by_d", align_bytes=64)
+        ts_listed = keep.tile([P, N], F32, name="ts_listed")
+        for j in range(PACK):
+            nc.vector.tensor_copy(w_by_d[:].rearrange("p (i j) -> p i j", j=PACK)[:, :, j], w_planes[j][:].indirect(offsets[:]))
+            if j == 0:
+                nc.vector.tensor_copy(ts_listed[:], ts_all[:].indirect(offsets[:]))
+        w_d = quantise("w_d", w_by_d[:], E4M3)
+
+        negated = keep.tile([P, ROW_PASSES * PACK], F32, name="negated")
+        guarded = keep.tile([P, ROW_PASSES * PACK], F32, name="guarded")
+        inverse = keep.tile([P, ROW_PASSES * PACK], F32, name="inverse")
+        flat = weights[:].rearrange("p g t -> p (g t)")
+        nc.vector.tensor_scalar(negated[:], flat, -1.0, None, ALU.mult)
+        nc.vector.scalar_tensor_tensor(guarded[:], flat, 0.0, flat, ALU.is_equal, ALU.add)
+        nc.vector.reciprocal(inverse[:], guarded[:])
+
+        def cast_x(g):
+            grouped = keep.tile([P, K_PASS * PACK], BF16, name="x_by_d%d" % g, align_bytes=64)
+            view = grouped[:].rearrange("p (t m j) -> p m j t", t=PACK, j=PACK)
+            for half in range(2):
+                nc.scalar.copy(
+                    view[:, half * 64 : (half + 1) * 64, :, :],
+                    x_raw[g][half][:].rearrange("p j (m t) -> p m j t", t=PACK),
+                )
+            return grouped
+
+        def cast_xm(g):
+            grouped = keep.tile([P, D * PACK], BF16, name="xm_by_r%d" % g, align_bytes=64)
+            nc.scalar.copy(
+                grouped[:].rearrange("p (c i t) -> p c t i", i=4, t=PACK),
+                xm_raw[g][:].rearrange("p t (c i) -> p c t i", i=4),
+            )
+            return grouped
+
+        def factor(g):
+            for t in range(PACK):
+                col = g * PACK + t
+                nc.vector.scalar_tensor_tensor(
+                    signed[g][:, t, :], signed[g][:, t, :], negated[:, col : col + 1], ts_listed[:], ALU.mult, ALU.mult
+                )
+
+        def scores(g, x_d):
+            sig = keep.tile([P, PACK, N], F32, name="sig%d" % g)
+            for t in range(PACK):
+                col = g * PACK + t
+                bank = psum.tile([P, N], F32, name="row_bank", bufs=3)
+                multiply(bank, x_d, t, w_d, True, True)
+                nc.vector.tensor_tensor(sig[:, t, :], bank[:], signed[g][:, t, :], ALU.mult)
+                nc.scalar.activation(sig[:, t, :], sig[:, t, :], ACT.Sigmoid, scale=inverse[:, col : col + 1])
+            return sig
+
+        def gradient(g, sig):
+            grouped = keep.tile([P, N * PACK], BF16, name="h_by_r%d" % g, align_bytes=64)
+            nc.vector.tensor_tensor(
+                grouped[:].rearrange("p (c i t) -> p c t i", i=4, t=PACK),
+                sig[:].rearrange("p t (c i) -> p c t i", i=4),
+                signed[g][:].rearrange("p t (c i) -> p c t i", i=4),
+                ALU.mult,
+            )
+            return grouped
+
+        def turn_h(g, grouped):
+            turned = keep.tile([P, K_PASS * PACK], BF16, name="h_by_i%d" % g, align_bytes=64)
+            view = turned[:].rearrange("s (u e p a) -> s u e p a", u=2, e=2, a=PACK)
+            for u in range(2):
+                nc.scalar.copy(view[:, u, :, :, :], turn(grouped, u).rearrange("s a p e -> s e p a"))
+            return turned
+
+        def rows_gradient(g, h_i, w_i):
+            result = raw.tile([P, PACK, D], F32, name="rows")
+            out_view = out_1[0].rearrange("(g p t) d -> g p t d", p=P, t=PACK)[g]
+            for t in range(PACK):
+                bank = psum.tile([P, D], F32, name="row_bank", bufs=3)
+                multiply(bank, h_i, t, w_i, True, True)
+                nc.scalar.copy(result[:, t, :], bank[:])
+                if t % 2 == 1:
+                    nc.sync.dma_start(out_view[:, t - 1 : t + 1, :], result[:, t - 1 : t + 1, :])
+
+        x_grouped0 = cast_x(0)
+        factor(0)
+        x_d0 = quantise("x_d0", x_grouped0[:], E4M3)
+        sig0 = scores(0, x_d0)
+        x_grouped1 = cast_x(1)
+        x_d1 = quantise("x_d1", x_grouped1[:], E4M3)
+        factor(1)
+        h0 = gradient(0, sig0)
+        sig1 = scores(1, x_d1)
+        h_r0 = quantise("h_r0", h0[:], E5M2)
+        xm_r0 = quantise("xm_r0", cast_xm(0)[:], E4M3)
+        xm_grouped1 = cast_xm(1)
+        h1 = gradient(1, sig1)
+        xm_r1 = quantise("xm_r1", xm_grouped1[:], E4M3)
+        h_r1 = quantise("h_r1", h1[:], E5M2)
+
+        sums = []
+        for j in range(D // P):
+            bank = psum.tile([P, N], F32, name="table_bank", bufs=2)
+            multiply(bank, xm_r0, j, h_r0, True, False)
+            multiply(bank, xm_r1, j, h_r1, False, True)
+            listed = keep.tile([P, N], F32, name="listed%d" % j)
+            nc.scalar.copy(listed[:], bank[:])
+            sums.append(listed)
+
+        w_by_i = keep.tile([P, D * PACK], BF16, name="w_by_i", align_bytes=64)
+        w_view = w_by_i[:].rearrange("s (p u e a) -> s u p e a", u=2, e=2, a=PACK)
+        for u in range(2):
+            nc.scalar.copy(w_view[:, u, :, :, :], turn(w_by_d, u).rearrange("s a p e -> s p e a"))
+        turned0 = turn_h(0, h0)
+        turned1 = turn_h(1, h1)
+
+        def scatter(j):
+            nc.vector.tensor_copy(windows[j][:].indirect(offsets[:]), sums[j][:])
+            nc.sync.dma_start(out_0[j * P : (j + 1) * P, :], windows[j][:])
+
+        w_i = quantise("w_i", w_by_i[:], E4M3)
+        h_i0 = quantise("h_i0", turned0[:], E5M2)
+        scatter(0)
+        rows_gradient(0, h_i0, w_i)
+        h_i1 = quantise("h_i1", turned1[:], E5M2)
+        scatter(1)
+        rows_gradient(1, h_i1, w_i)
+        scatter(2)
+        scatter(3)

@@ -9,6 +9,7 @@ BYTES = 4 * (2 * D * R + 2 * D * T + R * N + R + T + R * D) + 2 * 128 * (N // 16
 
 F32 = mybir.dt.float32
 BF16 = mybir.dt.bfloat16
+I32 = mybir.dt.int32
 U32 = mybir.dt.uint32
 U16 = mybir.dt.uint16
 U8 = mybir.dt.uint8
@@ -30,10 +31,17 @@ def tile_attend_gsig_wx_ts_kernel(tc, xT, wT, y, wt, ts, xm, offs, out_0, out_1)
         raw = ctx.enter_context(tc.tile_pool(name="raw", bufs=3))
         psum = ctx.enter_context(tc.psum_pool(name="psum", bufs=1))
 
-        def quantise(name, grouped, fmt):
-            codes = keep.tile([P, K_PASS], U32, name=name + "_codes", align_bytes=64)
+        def quantise(name, grouped, fmt, slot="", parts=1):
+            codes = keep.tile([P, K_PASS], U32, name=name + "_codes", tag=slot, align_bytes=64)
             scales = keep.tile([P, K_PASS], U8, name=name + "_scales", align_bytes=64)
-            nc.vector.quantize_mx(out=codes[:].bitcast(fmt), scales=scales[:], in_=grouped)
+            width = K_PASS // parts
+            for part in range(parts):
+                cols = slice(part * width, (part + 1) * width)
+                nc.vector.quantize_mx(
+                    out=codes[:, cols].bitcast(fmt),
+                    scales=scales[:, cols],
+                    in_=grouped[:, part * width * PACK : (part + 1) * width * PACK],
+                )
             return codes, scales, fmt
 
         def multiply(bank, stationary, q, moving, start, stop):
@@ -48,9 +56,9 @@ def tile_attend_gsig_wx_ts_kernel(tc, xT, wT, y, wt, ts, xm, offs, out_0, out_1)
                 stop=stop,
             )
 
-        def turn(grouped, u):
+        def turn(grouped, u, bank_name):
             words = grouped[:].bitcast(F32)
-            bank = psum.tile([P, PACK, P], F32, name="turn_bank", bufs=3)
+            bank = psum.tile([P, PACK, P], F32, name=bank_name)
             for place in range(PACK):
                 nc.tensor.transpose(bank[:, place, :], words[:, 2 * place + u : 2 * N : 2 * PACK], identity[:])
             return bank[:].rearrange("s a p -> s (a p)").bitcast(BF16).rearrange("s (a p e) -> s a p e", a=PACK, e=2)
@@ -58,51 +66,54 @@ def tile_attend_gsig_wx_ts_kernel(tc, xT, wT, y, wt, ts, xm, offs, out_0, out_1)
         offsets = keep.tile([P, N // 16], U16, name="offsets")
         nc.sync.dma_start(offsets[:], offs)
         ts_cols = keep.tile([P, T // P], F32, name="ts_cols")
-        nc.sync.dma_start(ts_cols[:], ts[0, :].rearrange("(n k) -> n k", k=T // P))
+        nc.scalar.dma_start(ts_cols[:], ts[0, :].rearrange("(n k) -> n k", k=T // P))
+        weights = keep.tile([P, ROW_PASSES, PACK], F32, name="weights")
+        nc.scalar.dma_start(weights[:], wt[0].rearrange("(g p t) o -> p g (t o)", p=P, t=PACK))
+        x_view = xT[0].rearrange("(p j) r -> p j r", j=PACK)
+        y_view = y[0].rearrange("(g p t) i -> g p t i", p=P, t=PACK)
+        xm_view = xm[0].rearrange("(g p t) d -> g p t d", p=P, t=PACK)
+
+        def load_x(g):
+            piece = keep.tile([P, PACK, K_PASS], F32, name="x_raw%d" % g, tag="sig%d" % (1 - g), align_bytes=64)
+            nc.sync.dma_start(piece[:], x_view[:, :, g * K_PASS : (g + 1) * K_PASS])
+            return piece
+
+        def load_y(g, half):
+            nc.sync.dma_start(signed[g][:, 2 * half : 2 * half + 2, :], y_view[g][:, 2 * half : 2 * half + 2, :])
+
+        def load_xm(g):
+            rows = raw.tile([P, PACK, D], F32, name="rows")
+            nc.sync.dma_start(rows[:], xm_view[g])
+            return rows
+
         w_planes = []
         for j in range(PACK):
             plane = keep.tile([P, T], F32, name="w_plane%d" % j)
             nc.sync.dma_start(plane[:], wT.rearrange("(p j) c -> p j c", j=PACK)[:, j, :])
             w_planes.append(plane)
-        weights = keep.tile([P, ROW_PASSES, PACK], F32, name="weights")
-        nc.sync.dma_start(weights[:], wt[0].rearrange("(g p t) o -> p g (t o)", p=P, t=PACK))
-        x_view = xT[0].rearrange("(p j) r -> p j r", j=PACK)
-        y_view = y[0].rearrange("(g p t) i -> g p t i", p=P, t=PACK)
-        xm_view = xm[0].rearrange("(g p t) d -> g p t d", p=P, t=PACK)
-        x_raw = []
-        signed = []
-        for g in range(ROW_PASSES):
-            halves = []
-            for half in range(2):
-                piece = keep.tile([P, PACK, K_PASS // 2], F32, name="x_raw%d%d" % (g, half))
-                c0 = g * K_PASS + half * (K_PASS // 2)
-                nc.sync.dma_start(piece[:], x_view[:, :, c0 : c0 + K_PASS // 2])
-                halves.append(piece)
-            x_raw.append(halves)
-            labels = keep.tile([P, PACK, N], F32, name="signed%d" % g)
-            for half in range(2):
-                nc.sync.dma_start(labels[:, 2 * half : 2 * half + 2, :], y_view[g][:, 2 * half : 2 * half + 2, :])
-            signed.append(labels)
-        xm_raw = []
-        for g in range(ROW_PASSES):
-            rows = raw.tile([P, PACK, D], F32, name="rows")
-            nc.sync.dma_start(rows[:], xm_view[g])
-            xm_raw.append(rows)
+        x_raw = [load_x(0)]
+        signed = [keep.tile([P, PACK, N], F32, name="signed%d" % g, tag="signed%d" % g, align_bytes=64) for g in range(ROW_PASSES)]
+        load_y(0, 0)
+        load_y(0, 1)
+        x_raw.append(load_x(1))
+        load_y(1, 0)
+        load_y(1, 1)
+        xm_raw = [load_xm(0), load_xm(1)]
 
         identity = keep.tile([P, P], F32, name="identity")
         make_identity(nc, identity[:])
         warm = keep.tile([P, 1], F32, name="warm")
         nc.scalar.activation(warm[:], identity[:, 0:1], ACT.Sigmoid)
         windows = []
-        for j in range(D // P):
+        for j in range(3):
             window = keep.tile([P, T], F32, name="window%d" % j)
-            nc.vector.memset(window[:], 0.0)
+            nc.vector.memset(window[:].bitcast(I32), 0)
             windows.append(window)
 
         ts_all = keep.tile([P, T], F32, name="ts_all")
         per = T // P
         for b in range(per // PACK):
-            bank = psum.tile([P, PACK, P], F32, name="turn_bank", bufs=3)
+            bank = psum.tile([P, PACK, P], F32, name="bank%d" % b)
             for kk in range(PACK):
                 k = PACK * b + kk
                 nc.tensor.transpose(bank[:, kk, :], ts_cols[:, k : k + 1].to_broadcast([P, P]), identity[:])
@@ -115,9 +126,9 @@ def tile_attend_gsig_wx_ts_kernel(tc, xT, wT, y, wt, ts, xm, offs, out_0, out_1)
         ts_listed = keep.tile([P, N], F32, name="ts_listed")
         for j in range(PACK):
             nc.vector.tensor_copy(w_by_d[:].rearrange("p (i j) -> p i j", j=PACK)[:, :, j], w_planes[j][:].indirect(offsets[:]))
-            if j == 0:
+            if j == 1:
                 nc.vector.tensor_copy(ts_listed[:], ts_all[:].indirect(offsets[:]))
-        w_d = quantise("w_d", w_by_d[:], E4M3)
+        w_d = quantise("w_d", w_by_d, E4M3)
 
         negated = keep.tile([P, ROW_PASSES * PACK], F32, name="negated")
         guarded = keep.tile([P, ROW_PASSES * PACK], F32, name="guarded")
@@ -127,110 +138,117 @@ def tile_attend_gsig_wx_ts_kernel(tc, xT, wT, y, wt, ts, xm, offs, out_0, out_1)
         nc.vector.scalar_tensor_tensor(guarded[:], flat, 0.0, flat, ALU.is_equal, ALU.add)
         nc.vector.reciprocal(inverse[:], guarded[:])
 
-        def cast_x(g):
+        def cast_x(g, copies):
             grouped = keep.tile([P, K_PASS * PACK], BF16, name="x_by_d%d" % g, align_bytes=64)
-            view = grouped[:].rearrange("p (t m j) -> p m j t", t=PACK, j=PACK)
-            for half in range(2):
-                nc.scalar.copy(
-                    view[:, half * 64 : (half + 1) * 64, :, :],
-                    x_raw[g][half][:].rearrange("p j (m t) -> p m j t", t=PACK),
-                )
+            dealt = grouped[:].rearrange("p (u e m j) -> p u m j e", u=2, e=2, j=PACK)
+            source = x_raw[g][:].rearrange("p j (m u e) -> p u m j e", u=2, e=2)
+            for u in range(2):
+                copies[u](dealt[:, u, :, :, :], source[:, u, :, :, :])
             return grouped
 
         def cast_xm(g):
-            grouped = keep.tile([P, D * PACK], BF16, name="xm_by_r%d" % g, align_bytes=64)
-            nc.scalar.copy(
-                grouped[:].rearrange("p (c i t) -> p c t i", i=4, t=PACK),
-                xm_raw[g][:].rearrange("p t (c i) -> p c t i", i=4),
-            )
+            grouped = keep.tile([P, D * PACK], BF16, name="xm_by_r%d" % g, tag="logits%d" % g, align_bytes=64)
+            woven = grouped[:].rearrange("p (c e t) -> p c t e", e=2, t=PACK)
+            source = xm_raw[g][:].rearrange("p t (c e) -> p c t e", e=2)
+            for half in range(2):
+                pairs = slice(half * D // 4, (half + 1) * D // 4)
+                nc.scalar.copy(woven[:, pairs, :, :], source[:, pairs, :, :])
             return grouped
 
-        def factor(g):
-            for t in range(PACK):
+        def factor(g, places):
+            for t in places:
                 col = g * PACK + t
                 nc.vector.scalar_tensor_tensor(
                     signed[g][:, t, :], signed[g][:, t, :], negated[:, col : col + 1], ts_listed[:], ALU.mult, ALU.mult
                 )
 
         def scores(g, x_d):
-            sig = keep.tile([P, PACK, N], F32, name="sig%d" % g)
+            sig = keep.tile([P, PACK, N], F32, name="sig%d" % g, tag="sig%d" % g, align_bytes=64)
+            logits = keep.tile([P, PACK, N], F32, name="logits%d" % g, tag="logits%d" % g, align_bytes=64)
             for t in range(PACK):
                 col = g * PACK + t
-                bank = psum.tile([P, N], F32, name="row_bank", bufs=3)
+                bank = psum.tile([P, N], F32, name="bank%d" % (PACK * g + t))
                 multiply(bank, x_d, t, w_d, True, True)
-                nc.vector.tensor_tensor(sig[:, t, :], bank[:], signed[g][:, t, :], ALU.mult)
-                nc.scalar.activation(sig[:, t, :], sig[:, t, :], ACT.Sigmoid, scale=inverse[:, col : col + 1])
+                nc.vector.tensor_tensor(logits[:, t, :], bank[:], signed[g][:, t, :], ALU.mult)
+                nc.scalar.activation(sig[:, t, :], logits[:, t, :], ACT.Sigmoid, scale=inverse[:, col : col + 1])
             return sig
 
         def gradient(g, sig):
             grouped = keep.tile([P, N * PACK], BF16, name="h_by_r%d" % g, align_bytes=64)
             nc.vector.tensor_tensor(
-                grouped[:].rearrange("p (c i t) -> p c t i", i=4, t=PACK),
-                sig[:].rearrange("p t (c i) -> p c t i", i=4),
-                signed[g][:].rearrange("p t (c i) -> p c t i", i=4),
+                grouped[:].rearrange("p (c e t) -> p c t e", e=2, t=PACK),
+                sig[:].rearrange("p t (c e) -> p c t e", e=2),
+                signed[g][:].rearrange("p t (c e) -> p c t e", e=2),
                 ALU.mult,
             )
             return grouped
 
-        def turn_h(g, grouped):
+        def turn_h(g, grouped, banks):
             turned = keep.tile([P, K_PASS * PACK], BF16, name="h_by_i%d" % g, align_bytes=64)
             view = turned[:].rearrange("s (u e p a) -> s u e p a", u=2, e=2, a=PACK)
             for u in range(2):
-                nc.scalar.copy(view[:, u, :, :, :], turn(grouped, u).rearrange("s a p e -> s e p a"))
+                nc.scalar.copy(view[:, u, :, :, :], turn(grouped, u, banks[u]).rearrange("s a p e -> s e p a"))
             return turned
 
-        def rows_gradient(g, h_i, w_i):
+        def rows_gradient(g, h_i, w_i, banks):
             result = raw.tile([P, PACK, D], F32, name="rows")
             out_view = out_1[0].rearrange("(g p t) d -> g p t d", p=P, t=PACK)[g]
             for t in range(PACK):
-                bank = psum.tile([P, D], F32, name="row_bank", bufs=3)
+                bank = psum.tile([P, D], F32, name=banks[t])
                 multiply(bank, h_i, t, w_i, True, True)
                 nc.scalar.copy(result[:, t, :], bank[:])
                 if t % 2 == 1:
-                    nc.sync.dma_start(out_view[:, t - 1 : t + 1, :], result[:, t - 1 : t + 1, :])
+                    nc.scalar.dma_start(out_view[:, t - 1 : t + 1, :], result[:, t - 1 : t + 1, :])
 
-        x_grouped0 = cast_x(0)
-        factor(0)
-        x_d0 = quantise("x_d0", x_grouped0[:], E4M3)
-        sig0 = scores(0, x_d0)
-        x_grouped1 = cast_x(1)
-        x_d1 = quantise("x_d1", x_grouped1[:], E4M3)
-        factor(1)
-        h0 = gradient(0, sig0)
-        sig1 = scores(1, x_d1)
-        h_r0 = quantise("h_r0", h0[:], E5M2)
-        xm_r0 = quantise("xm_r0", cast_xm(0)[:], E4M3)
-        xm_grouped1 = cast_xm(1)
-        h1 = gradient(1, sig1)
-        xm_r1 = quantise("xm_r1", xm_grouped1[:], E4M3)
-        h_r1 = quantise("h_r1", h1[:], E5M2)
-
-        sums = []
-        for j in range(D // P):
-            bank = psum.tile([P, N], F32, name="table_bank", bufs=2)
+        def table_open(j, bank_name):
+            bank = psum.tile([P, N], F32, name=bank_name)
             multiply(bank, xm_r0, j, h_r0, True, False)
+            return bank
+
+        def table_close(j, bank):
             multiply(bank, xm_r1, j, h_r1, False, True)
             listed = keep.tile([P, N], F32, name="listed%d" % j)
             nc.scalar.copy(listed[:], bank[:])
-            sums.append(listed)
+            return listed
 
+        def scatter(j, listed):
+            window = windows[j % len(windows)]
+            nc.vector.tensor_copy(window[:].indirect(offsets[:]), listed[:])
+            nc.sync.dma_start(out_0[j * P : (j + 1) * P, :], window[:])
+
+        x_d0 = quantise("x_d0", cast_x(0, (nc.vector.tensor_copy, nc.scalar.copy)), E4M3, parts=2)
         w_by_i = keep.tile([P, D * PACK], BF16, name="w_by_i", align_bytes=64)
         w_view = w_by_i[:].rearrange("s (p u e a) -> s u p e a", u=2, e=2, a=PACK)
         for u in range(2):
-            nc.scalar.copy(w_view[:, u, :, :, :], turn(w_by_d, u).rearrange("s a p e -> s p e a"))
-        turned0 = turn_h(0, h0)
-        turned1 = turn_h(1, h1)
-
-        def scatter(j):
-            nc.vector.tensor_copy(windows[j][:].indirect(offsets[:]), sums[j][:])
-            nc.sync.dma_start(out_0[j * P : (j + 1) * P, :], windows[j][:])
-
-        w_i = quantise("w_i", w_by_i[:], E4M3)
-        h_i0 = quantise("h_i0", turned0[:], E5M2)
-        scatter(0)
-        rows_gradient(0, h_i0, w_i)
-        h_i1 = quantise("h_i1", turned1[:], E5M2)
-        scatter(1)
-        rows_gradient(1, h_i1, w_i)
-        scatter(2)
-        scatter(3)
+            nc.scalar.copy(w_view[:, u, :, :, :], turn(w_by_d, u, "bank%d" % (6 + u)).rearrange("s a p e -> s p e a"))
+        x_grouped1 = cast_x(1, (nc.scalar.copy, nc.scalar.copy))
+        factor(0, range(PACK))
+        sig0 = scores(0, x_d0)
+        factor(1, range(2))
+        x_d1 = quantise("x_d1", x_grouped1, E4M3)
+        factor(1, range(2, PACK))
+        sig1 = scores(1, x_d1)
+        h0 = gradient(0, sig0)
+        xm_r0 = quantise("xm_r0", cast_xm(0), E4M3)
+        h_r0 = quantise("h_r0", h0, E5M2)
+        xm_grouped1 = cast_xm(1)
+        turned0 = turn_h(0, h0, ("bank0", "bank1"))
+        open0 = table_open(0, "bank4")
+        open1 = table_open(1, "bank5")
+        h1 = gradient(1, sig1)
+        xm_r1 = quantise("xm_r1", xm_grouped1, E4M3)
+        h_r1 = quantise("h_r1", h1, E5M2)
+        listed0 = table_close(0, open0)
+        listed1 = table_close(1, open1)
+        w_i = quantise("w_i", w_by_i, E4M3, "sig1")
+        h_i0 = quantise("h_i0", turned0, E5M2, "signed1")
+        scatter(0, listed0)
+        scatter(1, listed1)
+        rows_gradient(0, h_i0, w_i, ("bank6", "bank7", "bank2", "bank3"))
+        turned1 = turn_h(1, h1, ("bank4", "bank5"))
+        h_i1 = quantise("h_i1", turned1, E5M2)
+        listed2 = table_close(2, table_open(2, "bank4"))
+        listed3 = table_close(3, table_open(3, "bank5"))
+        rows_gradient(1, h_i1, w_i, ("bank0", "bank1", "bank6", "bank7"))
+        scatter(2, listed2)
+        scatter(3, listed3)

@@ -22,26 +22,22 @@ P = 128
 PACK = 4
 K_PASS = P * PACK
 ROW_PASSES = R // K_PASS
+X0_VECTOR = 80
 
 
 def tile_attend_gsig_wx_ts_kernel(tc, xT, wT, y, wt, ts, xm, offs, out_0, out_1):
     nc = tc.nc
     with ExitStack() as ctx:
         keep = ctx.enter_context(tc.tile_pool(name="keep", bufs=1))
-        raw = ctx.enter_context(tc.tile_pool(name="raw", bufs=3))
         psum = ctx.enter_context(tc.psum_pool(name="psum", bufs=1))
 
-        def quantise(name, grouped, fmt, slot="", parts=1):
-            codes = keep.tile([P, K_PASS], U32, name=name + "_codes", tag=slot, align_bytes=64)
-            scales = keep.tile([P, K_PASS], U8, name=name + "_scales", align_bytes=64)
-            width = K_PASS // parts
-            for part in range(parts):
-                cols = slice(part * width, (part + 1) * width)
-                nc.vector.quantize_mx(
-                    out=codes[:, cols].bitcast(fmt),
-                    scales=scales[:, cols],
-                    in_=grouped[:, part * width * PACK : (part + 1) * width * PACK],
-                )
+        def bank_tile(b, shape):
+            return psum.tile(shape, F32, name="bank%d" % b)
+
+        def quantise(name, grouped, fmt, width=K_PASS, slot=""):
+            codes = keep.tile([P, width], U32, name=name + "_codes", tag=slot, align_bytes=64)
+            scales = keep.tile([P, width], U8, name=name + "_scales", align_bytes=64)
+            nc.vector.quantize_mx(out=codes[:].bitcast(fmt), scales=scales[:], in_=grouped[:])
             return codes, scales, fmt
 
         def multiply(bank, stationary, q, moving, start, stop):
@@ -56,11 +52,11 @@ def tile_attend_gsig_wx_ts_kernel(tc, xT, wT, y, wt, ts, xm, offs, out_0, out_1)
                 stop=stop,
             )
 
-        def turn(grouped, u, bank_name):
+        def turn(grouped, u, b):
             words = grouped[:].bitcast(F32)
-            bank = psum.tile([P, PACK, P], F32, name=bank_name)
-            for place in range(PACK):
-                nc.tensor.transpose(bank[:, place, :], words[:, 2 * place + u : 2 * N : 2 * PACK], identity[:])
+            bank = bank_tile(b, [P, PACK, P])
+            for a in range(PACK):
+                nc.tensor.transpose(bank[:, a, :], words[:, 2 * P * a + u : 2 * P * (a + 1) : 2], identity[:])
             return bank[:].rearrange("s a p -> s (a p)").bitcast(BF16).rearrange("s (a p e) -> s a p e", a=PACK, e=2)
 
         offsets = keep.tile([P, N // 16], U16, name="offsets")
@@ -82,17 +78,17 @@ def tile_attend_gsig_wx_ts_kernel(tc, xT, wT, y, wt, ts, xm, offs, out_0, out_1)
             nc.sync.dma_start(signed[g][:, 2 * half : 2 * half + 2, :], y_view[g][:, 2 * half : 2 * half + 2, :])
 
         def load_xm(g):
-            rows = raw.tile([P, PACK, D], F32, name="rows")
+            rows = keep.tile([P, PACK, D], F32, name="xm_raw%d" % g)
             nc.sync.dma_start(rows[:], xm_view[g])
             return rows
 
         w_planes = []
         for j in range(PACK):
-            plane = keep.tile([P, T], F32, name="w_plane%d" % j)
+            plane = keep.tile([P, T], F32, name="w_plane%d" % j, tag="plane%d" % j)
             nc.sync.dma_start(plane[:], wT.rearrange("(p j) c -> p j c", j=PACK)[:, j, :])
             w_planes.append(plane)
         x_raw = [load_x(0)]
-        signed = [keep.tile([P, PACK, N], F32, name="signed%d" % g, tag="signed%d" % g, align_bytes=64) for g in range(ROW_PASSES)]
+        signed = [keep.tile([P, PACK, N], F32, name="signed%d" % g, align_bytes=64) for g in range(ROW_PASSES)]
         load_y(0, 0)
         load_y(0, 1)
         x_raw.append(load_x(1))
@@ -107,13 +103,13 @@ def tile_attend_gsig_wx_ts_kernel(tc, xT, wT, y, wt, ts, xm, offs, out_0, out_1)
         windows = []
         for j in range(3):
             window = keep.tile([P, T], F32, name="window%d" % j)
-            nc.vector.memset(window[:].bitcast(I32), 0)
+            nc.gpsimd.memset(window[:].bitcast(I32), 0)
             windows.append(window)
 
         ts_all = keep.tile([P, T], F32, name="ts_all")
         per = T // P
         for b in range(per // PACK):
-            bank = psum.tile([P, PACK, P], F32, name="bank%d" % b)
+            bank = bank_tile(b, [P, PACK, P])
             for kk in range(PACK):
                 k = PACK * b + kk
                 nc.tensor.transpose(bank[:, kk, :], ts_cols[:, k : k + 1].to_broadcast([P, P]), identity[:])
@@ -121,14 +117,6 @@ def tile_attend_gsig_wx_ts_kernel(tc, xT, wT, y, wt, ts, xm, offs, out_0, out_1)
                 ts_all[:].rearrange("p (n k) -> p n k", k=per)[:, :, PACK * b : PACK * (b + 1)],
                 bank[:].rearrange("p k n -> p n k"),
             )
-
-        w_by_d = keep.tile([P, N * PACK], BF16, name="w_by_d", align_bytes=64)
-        ts_listed = keep.tile([P, N], F32, name="ts_listed")
-        for j in range(PACK):
-            nc.vector.tensor_copy(w_by_d[:].rearrange("p (i j) -> p i j", j=PACK)[:, :, j], w_planes[j][:].indirect(offsets[:]))
-            if j == 1:
-                nc.vector.tensor_copy(ts_listed[:], ts_all[:].indirect(offsets[:]))
-        w_d = quantise("w_d", w_by_d, E4M3)
 
         negated = keep.tile([P, ROW_PASSES * PACK], F32, name="negated")
         guarded = keep.tile([P, ROW_PASSES * PACK], F32, name="guarded")
@@ -138,21 +126,29 @@ def tile_attend_gsig_wx_ts_kernel(tc, xT, wT, y, wt, ts, xm, offs, out_0, out_1)
         nc.vector.scalar_tensor_tensor(guarded[:], flat, 0.0, flat, ALU.is_equal, ALU.add)
         nc.vector.reciprocal(inverse[:], guarded[:])
 
-        def cast_x(g, copies):
+        w_by_d = keep.tile([P, N * PACK], BF16, name="w_by_d", align_bytes=64)
+        ts_listed = keep.tile([P, N], F32, name="ts_listed")
+        for j in range(PACK):
+            nc.vector.tensor_copy(
+                w_by_d[:].rearrange("p (a s j) -> p s a j", a=PACK, j=PACK)[:, :, :, j], w_planes[j][:].indirect(offsets[:])
+            )
+            if j == 1:
+                nc.vector.tensor_copy(ts_listed[:], ts_all[:].indirect(offsets[:]))
+        w_d = quantise("w_d", w_by_d, E4M3)
+
+        def cast_x(g, shares):
             grouped = keep.tile([P, K_PASS * PACK], BF16, name="x_by_d%d" % g, align_bytes=64)
-            dealt = grouped[:].rearrange("p (u e m j) -> p u m j e", u=2, e=2, j=PACK)
-            source = x_raw[g][:].rearrange("p j (m u e) -> p u m j e", u=2, e=2)
-            for u in range(2):
-                copies[u](dealt[:, u, :, :, :], source[:, u, :, :, :])
+            dealt = grouped[:].rearrange("p (t m j) -> p m j t", t=PACK, j=PACK)
+            source = x_raw[g][:].rearrange("p j (m t) -> p m j t", t=PACK)
+            for copy, lo, hi in shares:
+                copy(dealt[:, lo:hi, :, :], source[:, lo:hi, :, :])
             return grouped
 
-        def cast_xm(g):
-            grouped = keep.tile([P, D * PACK], BF16, name="xm_by_r%d" % g, tag="logits%d" % g, align_bytes=64)
-            woven = grouped[:].rearrange("p (c e t) -> p c t e", e=2, t=PACK)
-            source = xm_raw[g][:].rearrange("p t (c e) -> p c t e", e=2)
-            for half in range(2):
-                pairs = slice(half * D // 4, (half + 1) * D // 4)
-                nc.scalar.copy(woven[:, pairs, :, :], source[:, pairs, :, :])
+        def cast_xm(g, half, slot=""):
+            grouped = keep.tile([P, D // 2 * PACK], BF16, name="xm_by_r%d%d" % (g, half), tag=slot, align_bytes=64)
+            woven = grouped[:].rearrange("p (c e t) -> p c t e", e=PACK, t=PACK)
+            source = xm_raw[g][:, :, half * D // 2 : (half + 1) * D // 2].rearrange("p t (c e) -> p c t e", e=PACK)
+            nc.scalar.copy(woven, source)
             return grouped
 
         def factor(g, places):
@@ -167,18 +163,23 @@ def tile_attend_gsig_wx_ts_kernel(tc, xT, wT, y, wt, ts, xm, offs, out_0, out_1)
             logits = keep.tile([P, PACK, N], F32, name="logits%d" % g, tag="logits%d" % g, align_bytes=64)
             for t in range(PACK):
                 col = g * PACK + t
-                bank = psum.tile([P, N], F32, name="bank%d" % (PACK * g + t))
+                bank = bank_tile(PACK * g + t, [P, N])
                 multiply(bank, x_d, t, w_d, True, True)
-                nc.vector.tensor_tensor(logits[:, t, :], bank[:], signed[g][:, t, :], ALU.mult)
+                nc.vector.tensor_tensor(
+                    logits[:, t, :].rearrange("p (s a) -> p s a", a=PACK),
+                    bank[:].rearrange("p (a s) -> p s a", a=PACK),
+                    signed[g][:, t, :].rearrange("p (s a) -> p s a", a=PACK),
+                    ALU.mult,
+                )
                 nc.scalar.activation(sig[:, t, :], logits[:, t, :], ACT.Sigmoid, scale=inverse[:, col : col + 1])
             return sig
 
         def gradient(g, sig):
             grouped = keep.tile([P, N * PACK], BF16, name="h_by_r%d" % g, align_bytes=64)
             nc.vector.tensor_tensor(
-                grouped[:].rearrange("p (c e t) -> p c t e", e=2, t=PACK),
-                sig[:].rearrange("p t (c e) -> p c t e", e=2),
-                signed[g][:].rearrange("p t (c e) -> p c t e", e=2),
+                grouped[:].rearrange("p (a s t) -> p s t a", a=PACK, t=PACK),
+                sig[:].rearrange("p t (s a) -> p s t a", a=PACK),
+                signed[g][:].rearrange("p t (s a) -> p s t a", a=PACK),
                 ALU.mult,
             )
             return grouped
@@ -191,24 +192,24 @@ def tile_attend_gsig_wx_ts_kernel(tc, xT, wT, y, wt, ts, xm, offs, out_0, out_1)
             return turned
 
         def rows_gradient(g, h_i, w_i, banks):
-            result = raw.tile([P, PACK, D], F32, name="rows")
+            result = keep.tile([P, PACK, D], F32, name="rows%d" % g, tag="plane%d" % g)
             out_view = out_1[0].rearrange("(g p t) d -> g p t d", p=P, t=PACK)[g]
             for t in range(PACK):
-                bank = psum.tile([P, D], F32, name=banks[t])
+                bank = bank_tile(banks[t], [P, D])
                 multiply(bank, h_i, t, w_i, True, True)
                 nc.scalar.copy(result[:, t, :], bank[:])
                 if t % 2 == 1:
-                    nc.scalar.dma_start(out_view[:, t - 1 : t + 1, :], result[:, t - 1 : t + 1, :])
+                    nc.sync.dma_start(out_view[:, t - 1 : t + 1, :], result[:, t - 1 : t + 1, :])
 
-        def table_open(j, bank_name):
-            bank = psum.tile([P, N], F32, name=bank_name)
-            multiply(bank, xm_r0, j, h_r0, True, False)
+        def table_open(j, b):
+            bank = bank_tile(b, [P, N])
+            multiply(bank, xm_r[0][j // 2], j % 2, h_r0, True, False)
             return bank
 
         def table_close(j, bank):
-            multiply(bank, xm_r1, j, h_r1, False, True)
+            multiply(bank, xm_r[1][j // 2], j % 2, h_r1, False, True)
             listed = keep.tile([P, N], F32, name="listed%d" % j)
-            nc.scalar.copy(listed[:], bank[:])
+            nc.scalar.copy(listed[:].rearrange("p (s a) -> p s a", a=PACK), bank[:].rearrange("p (a s) -> p s a", a=PACK))
             return listed
 
         def scatter(j, listed):
@@ -216,39 +217,47 @@ def tile_attend_gsig_wx_ts_kernel(tc, xT, wT, y, wt, ts, xm, offs, out_0, out_1)
             nc.vector.tensor_copy(window[:].indirect(offsets[:]), listed[:])
             nc.sync.dma_start(out_0[j * P : (j + 1) * P, :], window[:])
 
-        x_d0 = quantise("x_d0", cast_x(0, (nc.vector.tensor_copy, nc.scalar.copy)), E4M3, parts=2)
+        xm_r = [[None, None], [None, None]]
+        x_grouped0 = cast_x(0, ((nc.vector.tensor_copy, 0, X0_VECTOR), (nc.scalar.copy, X0_VECTOR, P)))
         w_by_i = keep.tile([P, D * PACK], BF16, name="w_by_i", align_bytes=64)
         w_view = w_by_i[:].rearrange("s (p u e a) -> s u p e a", u=2, e=2, a=PACK)
         for u in range(2):
-            nc.scalar.copy(w_view[:, u, :, :, :], turn(w_by_d, u, "bank%d" % (6 + u)).rearrange("s a p e -> s p e a"))
-        x_grouped1 = cast_x(1, (nc.scalar.copy, nc.scalar.copy))
-        factor(0, range(PACK))
+            nc.scalar.copy(w_view[:, u, :, :, :], turn(w_by_d, u, 6 + u).rearrange("s a p e -> s p e a"))
+        x_grouped1 = cast_x(1, ((nc.scalar.copy, 0, P),))
+        factor(0, range(2))
+        x_d0 = quantise("x_d0", x_grouped0, E4M3)
+        factor(0, range(2, PACK))
         sig0 = scores(0, x_d0)
         factor(1, range(2))
         x_d1 = quantise("x_d1", x_grouped1, E4M3)
         factor(1, range(2, PACK))
         sig1 = scores(1, x_d1)
         h0 = gradient(0, sig0)
-        xm_r0 = quantise("xm_r0", cast_xm(0), E4M3)
-        h_r0 = quantise("h_r0", h0, E5M2)
-        xm_grouped1 = cast_xm(1)
-        turned0 = turn_h(0, h0, ("bank0", "bank1"))
-        open0 = table_open(0, "bank4")
-        open1 = table_open(1, "bank5")
+        xm_a0 = cast_xm(0, 0, "logits0")
+        xm_a1 = cast_xm(1, 0, "logits1")
+        turned0 = turn_h(0, h0, (0, 1))
+        xm_r[0][0] = quantise("xm_r00", xm_a0, E4M3, D // 2)
         h1 = gradient(1, sig1)
-        xm_r1 = quantise("xm_r1", xm_grouped1, E4M3)
+        h_r0 = quantise("h_r0", h0, E5M2)
+        open0 = table_open(0, 2)
+        open1 = table_open(1, 3)
+        xm_r[1][0] = quantise("xm_r10", xm_a1, E4M3, D // 2)
         h_r1 = quantise("h_r1", h1, E5M2)
         listed0 = table_close(0, open0)
+        w_i = quantise("w_i", w_by_i, E4M3, slot="sig1")
+        h_i0 = quantise("h_i0", turned0, E5M2)
+        xm_b0 = cast_xm(0, 1)
+        xm_b1 = cast_xm(1, 1)
         listed1 = table_close(1, open1)
-        w_i = quantise("w_i", w_by_i, E4M3, "sig1")
-        h_i0 = quantise("h_i0", turned0, E5M2, "signed1")
+        rows_gradient(0, h_i0, w_i, (4, 5, 6, 7))
         scatter(0, listed0)
+        xm_r[0][1] = quantise("xm_r01", xm_b0, E4M3, D // 2)
+        xm_r[1][1] = quantise("xm_r11", xm_b1, E4M3, D // 2)
+        turned1 = turn_h(1, h1, (0, 1))
         scatter(1, listed1)
-        rows_gradient(0, h_i0, w_i, ("bank6", "bank7", "bank2", "bank3"))
-        turned1 = turn_h(1, h1, ("bank4", "bank5"))
+        listed2 = table_close(2, table_open(2, 2))
+        listed3 = table_close(3, table_open(3, 3))
         h_i1 = quantise("h_i1", turned1, E5M2)
-        listed2 = table_close(2, table_open(2, "bank4"))
-        listed3 = table_close(3, table_open(3, "bank5"))
-        rows_gradient(1, h_i1, w_i, ("bank0", "bank1", "bank6", "bank7"))
+        rows_gradient(1, h_i1, w_i, (4, 5, 6, 7))
         scatter(2, listed2)
         scatter(3, listed3)

@@ -103,7 +103,7 @@ def tile_attend_gsig_wx_ts_kernel(tc, xT, wT, y, wt, ts, xm, offs, out_0, out_1)
         windows = []
         for j in range(3):
             window = keep.tile([P, T], F32, name="window%d" % j)
-            nc.gpsimd.memset(window[:].bitcast(I32), 0)
+            nc.vector.memset(window[:].bitcast(I32), 0)
             windows.append(window)
 
         ts_all = keep.tile([P, T], F32, name="ts_all")
@@ -199,7 +199,7 @@ def tile_attend_gsig_wx_ts_kernel(tc, xT, wT, y, wt, ts, xm, offs, out_0, out_1)
                 multiply(bank, h_i, t, w_i, True, True)
                 nc.scalar.copy(result[:, t, :], bank[:])
                 if t % 2 == 1:
-                    nc.sync.dma_start(out_view[:, t - 1 : t + 1, :], result[:, t - 1 : t + 1, :])
+                    nc.scalar.dma_start(out_view[:, t - 1 : t + 1, :], result[:, t - 1 : t + 1, :])
 
         def table_open(j, b):
             bank = bank_tile(b, [P, N])

@@ -61,8 +61,8 @@ def tile_attend_gsig_wx_ts_kernel(tc, xT, wT, y, wt, ts, xm, offs, out_0, out_1)
 
         offsets = keep.tile([P, N // 16], U16, name="offsets")
         nc.sync.dma_start(offsets[:], offs)
-        ts_cols = keep.tile([P, T // P], F32, name="ts_cols")
-        nc.scalar.dma_start(ts_cols[:], ts[0, :].rearrange("(n k) -> n k", k=T // P))
+        ts_row = keep.tile([P, T], F32, name="ts_row")
+        nc.gpsimd.memset(ts_row[:].bitcast(I32), 0)
         weights = keep.tile([P, ROW_PASSES, PACK], F32, name="weights")
         nc.scalar.dma_start(weights[:], wt[0].rearrange("(g p t) o -> p g (t o)", p=P, t=PACK))
         x_view = xT[0].rearrange("(p j) r -> p j r", j=PACK)
@@ -70,7 +70,7 @@ def tile_attend_gsig_wx_ts_kernel(tc, xT, wT, y, wt, ts, xm, offs, out_0, out_1)
         xm_view = xm[0].rearrange("(g p t) d -> g p t d", p=P, t=PACK)
 
         def load_x(g):
-            piece = keep.tile([P, PACK, K_PASS], F32, name="x_raw%d" % g, tag="sig%d" % (1 - g), align_bytes=64)
+            piece = keep.tile([P, PACK, K_PASS], F32, name="x_raw%d" % g, tag="sig0" if g else "w_by_i", align_bytes=64)
             nc.sync.dma_start(piece[:], x_view[:, :, g * K_PASS : (g + 1) * K_PASS])
             return piece
 
@@ -78,15 +78,17 @@ def tile_attend_gsig_wx_ts_kernel(tc, xT, wT, y, wt, ts, xm, offs, out_0, out_1)
             nc.sync.dma_start(signed[g][:, 2 * half : 2 * half + 2, :], y_view[g][:, 2 * half : 2 * half + 2, :])
 
         def load_xm(g):
-            rows = keep.tile([P, PACK, D], F32, name="xm_raw%d" % g)
+            rows = keep.tile([P, PACK, D], F32, name="xm_raw%d" % g, tag="xm_raw%d" % g)
             nc.sync.dma_start(rows[:], xm_view[g])
             return rows
 
         w_planes = []
         for j in range(PACK):
-            plane = keep.tile([P, T], F32, name="w_plane%d" % j, tag="plane%d" % j)
+            plane = keep.tile([P, T], F32, name="w_plane%d" % j, tag="plane%d" % j, align_bytes=64)
             nc.sync.dma_start(plane[:], wT.rearrange("(p j) c -> p j c", j=PACK)[:, j, :])
             w_planes.append(plane)
+            if j == 0:
+                nc.sync.dma_start(ts_row[0:1, :], ts[0:1, :])
         x_raw = [load_x(0)]
         signed = [keep.tile([P, PACK, N], F32, name="signed%d" % g, align_bytes=64) for g in range(ROW_PASSES)]
         load_y(0, 0)
@@ -106,18 +108,6 @@ def tile_attend_gsig_wx_ts_kernel(tc, xT, wT, y, wt, ts, xm, offs, out_0, out_1)
             nc.vector.memset(window[:].bitcast(I32), 0)
             windows.append(window)
 
-        ts_all = keep.tile([P, T], F32, name="ts_all")
-        per = T // P
-        for b in range(per // PACK):
-            bank = bank_tile(b, [P, PACK, P])
-            for kk in range(PACK):
-                k = PACK * b + kk
-                nc.tensor.transpose(bank[:, kk, :], ts_cols[:, k : k + 1].to_broadcast([P, P]), identity[:])
-            nc.scalar.copy(
-                ts_all[:].rearrange("p (n k) -> p n k", k=per)[:, :, PACK * b : PACK * (b + 1)],
-                bank[:].rearrange("p k n -> p n k"),
-            )
-
         negated = keep.tile([P, ROW_PASSES * PACK], F32, name="negated")
         guarded = keep.tile([P, ROW_PASSES * PACK], F32, name="guarded")
         inverse = keep.tile([P, ROW_PASSES * PACK], F32, name="inverse")
@@ -132,9 +122,20 @@ def tile_attend_gsig_wx_ts_kernel(tc, xT, wT, y, wt, ts, xm, offs, out_0, out_1)
             nc.vector.tensor_copy(
                 w_by_d[:].rearrange("p (a s j) -> p s a j", a=PACK, j=PACK)[:, :, :, j], w_planes[j][:].indirect(offsets[:])
             )
-            if j == 1:
-                nc.vector.tensor_copy(ts_listed[:], ts_all[:].indirect(offsets[:]))
+            if j == 0:
+                nc.vector.tensor_copy(ts_listed[:], ts_row[:].indirect(offsets[:]))
         w_d = quantise("w_d", w_by_d, E4M3)
+
+        ts_down = keep.tile([P, PACK], F32, name="ts_down")
+        for half in range(2):
+            bank = bank_tile(4 + half, [P, 2, P])
+            for c in range(2):
+                block = 2 * half + c
+                nc.tensor.transpose(bank[:, c, :], ts_listed[:, block * P : (block + 1) * P], identity[:])
+            nc.scalar.copy(ts_down[:, 2 * half : 2 * half + 2], bank[:, :, 0])
+        ts_bank = bank_tile(7, [P, N])
+        for c in range(PACK):
+            nc.tensor.transpose(ts_bank[:, c * P : (c + 1) * P], ts_down[:, c : c + 1].to_broadcast([P, P]), identity[:])
 
         def cast_x(g, shares):
             grouped = keep.tile([P, K_PASS * PACK], BF16, name="x_by_d%d" % g, align_bytes=64)
@@ -144,26 +145,24 @@ def tile_attend_gsig_wx_ts_kernel(tc, xT, wT, y, wt, ts, xm, offs, out_0, out_1)
                 copy(dealt[:, lo:hi, :, :], source[:, lo:hi, :, :])
             return grouped
 
-        def cast_xm(g, half, slot=""):
-            grouped = keep.tile([P, D // 2 * PACK], BF16, name="xm_by_r%d%d" % (g, half), tag=slot, align_bytes=64)
-            woven = grouped[:].rearrange("p (c e t) -> p c t e", e=PACK, t=PACK)
+        def cast_xm(grouped, g, half):
+            woven = grouped.rearrange("p (c e t) -> p c t e", e=PACK, t=PACK)
             source = xm_raw[g][:, :, half * D // 2 : (half + 1) * D // 2].rearrange("p t (c e) -> p c t e", e=PACK)
             nc.scalar.copy(woven, source)
-            return grouped
 
         def factor(g, places):
             for t in places:
                 col = g * PACK + t
                 nc.vector.scalar_tensor_tensor(
-                    signed[g][:, t, :], signed[g][:, t, :], negated[:, col : col + 1], ts_listed[:], ALU.mult, ALU.mult
+                    signed[g][:, t, :], signed[g][:, t, :], negated[:, col : col + 1], ts_bank[:], ALU.mult, ALU.mult
                 )
 
-        def scores(g, x_d):
+        def scores(g, x_d, banks):
             sig = keep.tile([P, PACK, N], F32, name="sig%d" % g, tag="sig%d" % g, align_bytes=64)
             logits = keep.tile([P, PACK, N], F32, name="logits%d" % g, tag="logits%d" % g, align_bytes=64)
             for t in range(PACK):
                 col = g * PACK + t
-                bank = bank_tile(PACK * g + t, [P, N])
+                bank = bank_tile(banks[t], [P, N])
                 multiply(bank, x_d, t, w_d, True, True)
                 nc.vector.tensor_tensor(
                     logits[:, t, :].rearrange("p (s a) -> p s a", a=PACK),
@@ -185,14 +184,14 @@ def tile_attend_gsig_wx_ts_kernel(tc, xT, wT, y, wt, ts, xm, offs, out_0, out_1)
             return grouped
 
         def turn_h(g, grouped, banks):
-            turned = keep.tile([P, K_PASS * PACK], BF16, name="h_by_i%d" % g, align_bytes=64)
+            turned = keep.tile([P, K_PASS * PACK], BF16, name="h_by_i%d" % g, tag="h_by_i%d" % g, align_bytes=64)
             view = turned[:].rearrange("s (u e p a) -> s u e p a", u=2, e=2, a=PACK)
             for u in range(2):
                 nc.scalar.copy(view[:, u, :, :, :], turn(grouped, u, banks[u]).rearrange("s a p e -> s e p a"))
             return turned
 
         def rows_gradient(g, h_i, w_i, banks):
-            result = keep.tile([P, PACK, D], F32, name="rows%d" % g, tag="plane%d" % g)
+            result = keep.tile([P, PACK, D], F32, name="rows%d" % g, tag="plane%d" % g, align_bytes=64)
             out_view = out_1[0].rearrange("(g p t) d -> g p t d", p=P, t=PACK)[g]
             for t in range(PACK):
                 bank = bank_tile(banks[t], [P, D])
@@ -201,14 +200,11 @@ def tile_attend_gsig_wx_ts_kernel(tc, xT, wT, y, wt, ts, xm, offs, out_0, out_1)
                 if t % 2 == 1:
                     nc.scalar.dma_start(out_view[:, t - 1 : t + 1, :], result[:, t - 1 : t + 1, :])
 
-        def table_open(j, b):
+        def table_gradient(j, first, second, b):
             bank = bank_tile(b, [P, N])
-            multiply(bank, xm_r[0][j // 2], j % 2, h_r0, True, False)
-            return bank
-
-        def table_close(j, bank):
-            multiply(bank, xm_r[1][j // 2], j % 2, h_r1, False, True)
-            listed = keep.tile([P, N], F32, name="listed%d" % j)
+            multiply(bank, first[0], first[1], h_r0, True, False)
+            multiply(bank, second[0], second[1], h_r1, False, True)
+            listed = keep.tile([P, N], F32, name="listed%d" % j, tag="xm_raw1" if j == 1 else "")
             nc.scalar.copy(listed[:].rearrange("p (s a) -> p s a", a=PACK), bank[:].rearrange("p (a s) -> p s a", a=PACK))
             return listed
 
@@ -217,47 +213,46 @@ def tile_attend_gsig_wx_ts_kernel(tc, xT, wT, y, wt, ts, xm, offs, out_0, out_1)
             nc.vector.tensor_copy(window[:].indirect(offsets[:]), listed[:])
             nc.sync.dma_start(out_0[j * P : (j + 1) * P, :], window[:])
 
-        xm_r = [[None, None], [None, None]]
         x_grouped0 = cast_x(0, ((nc.vector.tensor_copy, 0, X0_VECTOR), (nc.scalar.copy, X0_VECTOR, P)))
-        w_by_i = keep.tile([P, D * PACK], BF16, name="w_by_i", align_bytes=64)
+        w_by_i = keep.tile([P, D * PACK], BF16, name="w_by_i", tag="w_by_i", align_bytes=64)
         w_view = w_by_i[:].rearrange("s (p u e a) -> s u p e a", u=2, e=2, a=PACK)
         for u in range(2):
-            nc.scalar.copy(w_view[:, u, :, :, :], turn(w_by_d, u, 6 + u).rearrange("s a p e -> s p e a"))
+            nc.scalar.copy(w_view[:, u, :, :, :], turn(w_by_d, u, 4 + u).rearrange("s a p e -> s p e a"))
         x_grouped1 = cast_x(1, ((nc.scalar.copy, 0, P),))
         factor(0, range(2))
         x_d0 = quantise("x_d0", x_grouped0, E4M3)
         factor(0, range(2, PACK))
-        sig0 = scores(0, x_d0)
+        sig0 = scores(0, x_d0, (0, 1, 2, 3))
         factor(1, range(2))
         x_d1 = quantise("x_d1", x_grouped1, E4M3)
         factor(1, range(2, PACK))
-        sig1 = scores(1, x_d1)
+        xm_low = keep.tile([P, D * PACK], BF16, name="xm_low", tag="logits0", align_bytes=64)
+        cast_xm(xm_low[:, : 2 * D], 0, 0)
+        sig1 = scores(1, x_d1, (4, 5, 6, 0))
         h0 = gradient(0, sig0)
-        xm_a0 = cast_xm(0, 0, "logits0")
-        xm_a1 = cast_xm(1, 0, "logits1")
-        turned0 = turn_h(0, h0, (0, 1))
-        xm_r[0][0] = quantise("xm_r00", xm_a0, E4M3, D // 2)
+        cast_xm(xm_low[:, 2 * D :], 1, 0)
+        turned0 = turn_h(0, h0, (1, 2))
         h1 = gradient(1, sig1)
         h_r0 = quantise("h_r0", h0, E5M2)
-        open0 = table_open(0, 2)
-        open1 = table_open(1, 3)
-        xm_r[1][0] = quantise("xm_r10", xm_a1, E4M3, D // 2)
+        xm_r_low = quantise("xm_r_low", xm_low, E4M3)
         h_r1 = quantise("h_r1", h1, E5M2)
-        listed0 = table_close(0, open0)
+        xm_high0 = keep.tile([P, 2 * D], BF16, name="xm_high0", tag="logits1", align_bytes=64)
+        cast_xm(xm_high0[:], 0, 1)
+        listed0 = table_gradient(0, (xm_r_low, 0), (xm_r_low, 2), 3)
         w_i = quantise("w_i", w_by_i, E4M3, slot="sig1")
         h_i0 = quantise("h_i0", turned0, E5M2)
-        xm_b0 = cast_xm(0, 1)
-        xm_b1 = cast_xm(1, 1)
-        listed1 = table_close(1, open1)
-        rows_gradient(0, h_i0, w_i, (4, 5, 6, 7))
+        xm_high1 = keep.tile([P, 2 * D], BF16, name="xm_high1", tag="h_by_i0", align_bytes=64)
+        cast_xm(xm_high1[:], 1, 1)
+        listed1 = table_gradient(1, (xm_r_low, 1), (xm_r_low, 3), 7)
+        rows_gradient(0, h_i0, w_i, (4, 5, 6, 0))
         scatter(0, listed0)
-        xm_r[0][1] = quantise("xm_r01", xm_b0, E4M3, D // 2)
-        xm_r[1][1] = quantise("xm_r11", xm_b1, E4M3, D // 2)
-        turned1 = turn_h(1, h1, (0, 1))
+        xm_r_high0 = quantise("xm_r_high0", xm_high0, E4M3, D // 2)
+        xm_r_high1 = quantise("xm_r_high1", xm_high1, E4M3, D // 2)
+        turned1 = turn_h(1, h1, (3, 7))
         scatter(1, listed1)
-        listed2 = table_close(2, table_open(2, 2))
-        listed3 = table_close(3, table_open(3, 3))
         h_i1 = quantise("h_i1", turned1, E5M2)
-        rows_gradient(1, h_i1, w_i, (4, 5, 6, 7))
+        listed2 = table_gradient(2, (xm_r_high0, 0), (xm_r_high1, 0), 3)
+        listed3 = table_gradient(3, (xm_r_high0, 1), (xm_r_high1, 1), 7)
+        rows_gradient(1, h_i1, w_i, (4, 5, 6, 0))
         scatter(2, listed2)
         scatter(3, listed3)

@@ -103,10 +103,14 @@ def tile_attend_gsig_wx_ts_kernel(tc, xT, wT, y, wt, ts, xm, offs, out_0, out_1)
         warm = keep.tile([P, 1], F32, name="warm")
         nc.scalar.activation(warm[:], identity[:, 0:1], ACT.Sigmoid)
         windows = []
-        for j in range(3):
-            window = keep.tile([P, T], F32, name="window%d" % j)
+
+        def clear_window():
+            window = keep.tile([P, T], F32, name="window%d" % len(windows))
             nc.vector.memset(window[:].bitcast(I32), 0)
             windows.append(window)
+
+        for count in range(3):
+            clear_window()
 
         negated = keep.tile([P, ROW_PASSES * PACK], F32, name="negated")
         guarded = keep.tile([P, ROW_PASSES * PACK], F32, name="guarded")
@@ -138,7 +142,7 @@ def tile_attend_gsig_wx_ts_kernel(tc, xT, wT, y, wt, ts, xm, offs, out_0, out_1)
             nc.tensor.transpose(ts_bank[:, c * P : (c + 1) * P], ts_down[:, c : c + 1].to_broadcast([P, P]), identity[:])
 
         def cast_x(g, shares):
-            grouped = keep.tile([P, K_PASS * PACK], BF16, name="x_by_d%d" % g, align_bytes=64)
+            grouped = keep.tile([P, K_PASS * PACK], BF16, name="x_by_d%d" % g, tag="x_by_d%d" % g, align_bytes=64)
             dealt = grouped[:].rearrange("p (t m j) -> p m j t", t=PACK, j=PACK)
             source = x_raw[g][:].rearrange("p j (m t) -> p m j t", t=PACK)
             for copy, lo, hi in shares:
@@ -200,11 +204,11 @@ def tile_attend_gsig_wx_ts_kernel(tc, xT, wT, y, wt, ts, xm, offs, out_0, out_1)
                 if t % 2 == 1:
                     nc.scalar.dma_start(out_view[:, t - 1 : t + 1, :], result[:, t - 1 : t + 1, :])
 
-        def table_gradient(j, first, second, b):
+        def table_gradient(j, xm_r, b):
             bank = bank_tile(b, [P, N])
-            multiply(bank, first[0], first[1], h_r0, True, False)
-            multiply(bank, second[0], second[1], h_r1, False, True)
-            listed = keep.tile([P, N], F32, name="listed%d" % j, tag="xm_raw1" if j == 1 else "")
+            multiply(bank, xm_r, j % 2, h_r0, True, False)
+            multiply(bank, xm_r, 2 + j % 2, h_r1, False, True)
+            listed = keep.tile([P, N], F32, name="listed%d" % j)
             nc.scalar.copy(listed[:].rearrange("p (s a) -> p s a", a=PACK), bank[:].rearrange("p (a s) -> p s a", a=PACK))
             return listed
 
@@ -236,23 +240,21 @@ def tile_attend_gsig_wx_ts_kernel(tc, xT, wT, y, wt, ts, xm, offs, out_0, out_1)
         h_r0 = quantise("h_r0", h0, E5M2)
         xm_r_low = quantise("xm_r_low", xm_low, E4M3)
         h_r1 = quantise("h_r1", h1, E5M2)
-        xm_high0 = keep.tile([P, 2 * D], BF16, name="xm_high0", tag="logits1", align_bytes=64)
-        cast_xm(xm_high0[:], 0, 1)
-        listed0 = table_gradient(0, (xm_r_low, 0), (xm_r_low, 2), 3)
+        xm_high = keep.tile([P, D * PACK], BF16, name="xm_high", tag="logits1", align_bytes=64)
+        cast_xm(xm_high[:, : 2 * D], 0, 1)
+        cast_xm(xm_high[:, 2 * D :], 1, 1)
+        listed0 = table_gradient(0, xm_r_low, 3)
         w_i = quantise("w_i", w_by_i, E4M3, slot="sig1")
         h_i0 = quantise("h_i0", turned0, E5M2)
-        xm_high1 = keep.tile([P, 2 * D], BF16, name="xm_high1", tag="h_by_i0", align_bytes=64)
-        cast_xm(xm_high1[:], 1, 1)
-        listed1 = table_gradient(1, (xm_r_low, 1), (xm_r_low, 3), 7)
+        xm_r_high = quantise("xm_r_high", xm_high, E4M3)
         rows_gradient(0, h_i0, w_i, (4, 5, 6, 0))
+        listed1 = table_gradient(1, xm_r_low, 5)
         scatter(0, listed0)
-        xm_r_high0 = quantise("xm_r_high0", xm_high0, E4M3, D // 2)
-        xm_r_high1 = quantise("xm_r_high1", xm_high1, E4M3, D // 2)
-        turned1 = turn_h(1, h1, (3, 7))
+        turned1 = turn_h(1, h1, (3, 4))
         scatter(1, listed1)
         h_i1 = quantise("h_i1", turned1, E5M2)
-        listed2 = table_gradient(2, (xm_r_high0, 0), (xm_r_high1, 0), 3)
-        listed3 = table_gradient(3, (xm_r_high0, 1), (xm_r_high1, 1), 7)
-        rows_gradient(1, h_i1, w_i, (4, 5, 6, 0))
+        listed2 = table_gradient(2, xm_r_high, 3)
+        listed3 = table_gradient(3, xm_r_high, 4)
+        rows_gradient(1, h_i1, w_i, (1, 2, 6, 0))
         scatter(2, listed2)
         scatter(3, listed3)

@@ -34,9 +34,9 @@ def tile_attend_gsig_wx_ts_kernel(tc, xT, wT, y, wt, ts, xm, offs, out_0, out_1)
         def bank_tile(b, shape):
             return psum.tile(shape, F32, name="bank%d" % b)
 
-        def quantise(name, grouped, fmt, width=K_PASS, slot=""):
-            codes = keep.tile([P, width], U32, name=name + "_codes", tag=slot, align_bytes=64)
-            scales = keep.tile([P, width], U8, name=name + "_scales", align_bytes=64)
+        def quantise(name, grouped, fmt, slot=""):
+            codes = keep.tile([P, K_PASS], U32, name=name + "_codes", tag=slot, align_bytes=64)
+            scales = keep.tile([P, K_PASS], U8, name=name + "_scales", align_bytes=64)
             nc.vector.quantize_mx(out=codes[:].bitcast(fmt), scales=scales[:], in_=grouped[:])
             return codes, scales, fmt
 
@@ -194,15 +194,15 @@ def tile_attend_gsig_wx_ts_kernel(tc, xT, wT, y, wt, ts, xm, offs, out_0, out_1)
                 nc.scalar.copy(view[:, u, :, :, :], turn(grouped, u, banks[u]).rearrange("s a p e -> s e p a"))
             return turned
 
-        def rows_gradient(g, h_i, w_i, banks):
-            result = keep.tile([P, PACK, D], F32, name="rows%d" % g, tag="plane%d" % g, align_bytes=64)
+        def rows_gradient(g, h_i, w_i, places, banks, per_store):
             out_view = out_1[0].rearrange("(g p t) d -> g p t d", p=P, t=PACK)[g]
-            for t in range(PACK):
+            for t in places:
                 bank = bank_tile(banks[t], [P, D])
                 multiply(bank, h_i, t, w_i, True, True)
-                nc.scalar.copy(result[:, t, :], bank[:])
-                if t % 2 == 1:
-                    nc.scalar.dma_start(out_view[:, t - 1 : t + 1, :], result[:, t - 1 : t + 1, :])
+                nc.scalar.copy(results[g][:, t, :], bank[:])
+                if (t + 1) % per_store == 0:
+                    done = slice(t + 1 - per_store, t + 1)
+                    nc.scalar.dma_start(out_view[:, done, :], results[g][:, done, :])
 
         def table_gradient(j, xm_r, b):
             bank = bank_tile(b, [P, N])
@@ -247,14 +247,16 @@ def tile_attend_gsig_wx_ts_kernel(tc, xT, wT, y, wt, ts, xm, offs, out_0, out_1)
         w_i = quantise("w_i", w_by_i, E4M3, slot="sig1")
         h_i0 = quantise("h_i0", turned0, E5M2)
         xm_r_high = quantise("xm_r_high", xm_high, E4M3)
-        rows_gradient(0, h_i0, w_i, (4, 5, 6, 0))
-        listed1 = table_gradient(1, xm_r_low, 5)
+        results = [keep.tile([P, PACK, D], F32, name="rows%d" % g, tag="plane%d" % g, align_bytes=64) for g in range(ROW_PASSES)]
+        rows_gradient(0, h_i0, w_i, range(3), (4, 5, 6, 0), 1)
+        listed1 = table_gradient(1, xm_r_low, 4)
+        rows_gradient(0, h_i0, w_i, range(3, PACK), (4, 5, 6, 0), 1)
         scatter(0, listed0)
-        turned1 = turn_h(1, h1, (3, 4))
+        turned1 = turn_h(1, h1, (3, 5))
         scatter(1, listed1)
         h_i1 = quantise("h_i1", turned1, E5M2)
         listed2 = table_gradient(2, xm_r_high, 3)
-        listed3 = table_gradient(3, xm_r_high, 4)
-        rows_gradient(1, h_i1, w_i, (1, 2, 6, 0))
+        listed3 = table_gradient(3, xm_r_high, 5)
+        rows_gradient(1, h_i1, w_i, range(PACK), (1, 2, 6, 0), 2)
         scatter(2, listed2)
         scatter(3, listed3)

@@ -34,10 +34,16 @@ def tile_attend_gsig_wx_ts_kernel(tc, xT, wT, y, wt, ts, xm, offs, out_0, out_1)
         def bank_tile(b, shape):
             return psum.tile(shape, F32, name="bank%d" % b)
 
-        def quantise(name, grouped, fmt, slot=""):
+        def quantise(name, grouped, fmt, slot="", parts=1):
             codes = keep.tile([P, K_PASS], U32, name=name + "_codes", tag=slot, align_bytes=64)
             scales = keep.tile([P, K_PASS], U8, name=name + "_scales", align_bytes=64)
-            nc.vector.quantize_mx(out=codes[:].bitcast(fmt), scales=scales[:], in_=grouped[:])
+            width = K_PASS // parts
+            for lo in range(0, K_PASS, width):
+                nc.vector.quantize_mx(
+                    out=codes[:, lo : lo + width].bitcast(fmt),
+                    scales=scales[:, lo : lo + width],
+                    in_=grouped[:, lo * PACK : (lo + width) * PACK],
+                )
             return codes, scales, fmt
 
         def multiply(bank, stationary, q, moving, start, stop):
@@ -194,15 +200,14 @@ def tile_attend_gsig_wx_ts_kernel(tc, xT, wT, y, wt, ts, xm, offs, out_0, out_1)
                 nc.scalar.copy(view[:, u, :, :, :], turn(grouped, u, banks[u]).rearrange("s a p e -> s e p a"))
             return turned
 
-        def rows_gradient(g, h_i, w_i, places, banks, per_store):
+        def rows_gradient(g, h_i, w_i, t, b):
+            bank = bank_tile(b, [P, D])
+            multiply(bank, h_i, t, w_i, True, True)
+            nc.scalar.copy(results[g][:, t, :], bank[:])
+
+        def store_rows(g, lo, hi):
             out_view = out_1[0].rearrange("(g p t) d -> g p t d", p=P, t=PACK)[g]
-            for t in places:
-                bank = bank_tile(banks[t], [P, D])
-                multiply(bank, h_i, t, w_i, True, True)
-                nc.scalar.copy(results[g][:, t, :], bank[:])
-                if (t + 1) % per_store == 0:
-                    done = slice(t + 1 - per_store, t + 1)
-                    nc.scalar.dma_start(out_view[:, done, :], results[g][:, done, :])
+            nc.scalar.dma_start(out_view[:, lo:hi, :], results[g][:, lo:hi, :])
 
         def table_gradient(j, xm_r, b):
             bank = bank_tile(b, [P, N])
@@ -245,18 +250,24 @@ def tile_attend_gsig_wx_ts_kernel(tc, xT, wT, y, wt, ts, xm, offs, out_0, out_1)
         cast_xm(xm_high[:, 2 * D :], 1, 1)
         listed0 = table_gradient(0, xm_r_low, 3)
         w_i = quantise("w_i", w_by_i, E4M3, slot="sig1")
-        h_i0 = quantise("h_i0", turned0, E5M2)
+        h_i0 = quantise("h_i0", turned0, E5M2, parts=2)
         xm_r_high = quantise("xm_r_high", xm_high, E4M3)
         results = [keep.tile([P, PACK, D], F32, name="rows%d" % g, tag="plane%d" % g, align_bytes=64) for g in range(ROW_PASSES)]
-        rows_gradient(0, h_i0, w_i, range(3), (4, 5, 6, 0), 1)
+        for t, b in enumerate((4, 5, 6, 0)):
+            rows_gradient(0, h_i0, w_i, t, b)
+            if t > 0:
+                store_rows(0, t - 1, t)
         listed1 = table_gradient(1, xm_r_low, 4)
-        rows_gradient(0, h_i0, w_i, range(3, PACK), (4, 5, 6, 0), 1)
+        store_rows(0, PACK - 1, PACK)
         scatter(0, listed0)
         turned1 = turn_h(1, h1, (3, 5))
         scatter(1, listed1)
         h_i1 = quantise("h_i1", turned1, E5M2)
         listed2 = table_gradient(2, xm_r_high, 3)
         listed3 = table_gradient(3, xm_r_high, 5)
-        rows_gradient(1, h_i1, w_i, range(PACK), (1, 2, 6, 0), 2)
+        for t, b in enumerate((1, 2, 6, 0)):
+            rows_gradient(1, h_i1, w_i, t, b)
+            if t % 2 == 1:
+                store_rows(1, t - 1, t + 1)
         scatter(2, listed2)
         scatter(3, listed3)

@@ -23,6 +23,7 @@ PACK = 4
 K_PASS = P * PACK
 ROW_PASSES = R // K_PASS
 X0_VECTOR = 80
+X1_VECTOR = 48
 
 
 def tile_attend_gsig_wx_ts_kernel(tc, xT, wT, y, wt, ts, xm, offs, out_0, out_1):
@@ -34,11 +35,11 @@ def tile_attend_gsig_wx_ts_kernel(tc, xT, wT, y, wt, ts, xm, offs, out_0, out_1)
         def bank_tile(b, shape):
             return psum.tile(shape, F32, name="bank%d" % b)
 
-        def quantise(name, grouped, fmt, slot="", parts=1):
-            codes = keep.tile([P, K_PASS], U32, name=name + "_codes", tag=slot, align_bytes=64)
-            scales = keep.tile([P, K_PASS], U8, name=name + "_scales", align_bytes=64)
-            width = K_PASS // parts
-            for lo in range(0, K_PASS, width):
+        def quantise(name, grouped, fmt, slot="", parts=1, words=K_PASS):
+            codes = keep.tile([P, words], U32, name=name + "_codes", tag=slot, align_bytes=64)
+            scales = keep.tile([P, words], U8, name=name + "_scales", align_bytes=64)
+            width = words // parts
+            for lo in range(0, words, width):
                 nc.vector.quantize_mx(
                     out=codes[:, lo : lo + width].bitcast(fmt),
                     scales=scales[:, lo : lo + width],
@@ -80,8 +81,11 @@ def tile_attend_gsig_wx_ts_kernel(tc, xT, wT, y, wt, ts, xm, offs, out_0, out_1)
             nc.sync.dma_start(piece[:], x_view[:, :, g * K_PASS : (g + 1) * K_PASS])
             return piece
 
-        def load_y(g, half):
-            nc.sync.dma_start(signed[g][:, 2 * half : 2 * half + 2, :], y_view[g][:, 2 * half : 2 * half + 2, :])
+        def load_y(g):
+            nc.sync.dma_start(signed[g][:, 0:2, :], y_view[g][:, 0:2, :])
+            late = keep.tile([P, 2, N], F32, name="late_signs%d" % g, align_bytes=64)
+            nc.sync.dma_start(late[:], y_view[g][:, 2:PACK, :])
+            return late
 
         def load_xm(g):
             rows = keep.tile([P, PACK, D], F32, name="xm_raw%d" % g, tag="xm_raw%d" % g)
@@ -96,12 +100,11 @@ def tile_attend_gsig_wx_ts_kernel(tc, xT, wT, y, wt, ts, xm, offs, out_0, out_1)
             if j == 0:
                 nc.sync.dma_start(ts_row[0:1, :], ts[0:1, :])
         x_raw = [load_x(0)]
-        signed = [keep.tile([P, PACK, N], F32, name="signed%d" % g, align_bytes=64) for g in range(ROW_PASSES)]
-        load_y(0, 0)
-        load_y(0, 1)
+        signed_rows = [keep.tile([P, PACK * N], F32, name="signed%d" % g, align_bytes=64) for g in range(ROW_PASSES)]
+        signed = [rows[:].rearrange("p (t i) -> p t i", t=PACK) for rows in signed_rows]
+        late_signs = [load_y(0)]
         x_raw.append(load_x(1))
-        load_y(1, 0)
-        load_y(1, 1)
+        late_signs.append(load_y(1))
         xm_raw = [load_xm(0), load_xm(1)]
 
         identity = keep.tile([P, P], F32, name="identity")
@@ -147,9 +150,15 @@ def tile_attend_gsig_wx_ts_kernel(tc, xT, wT, y, wt, ts, xm, offs, out_0, out_1)
         for c in range(PACK):
             nc.tensor.transpose(ts_bank[:, c * P : (c + 1) * P], ts_down[:, c : c + 1].to_broadcast([P, P]), identity[:])
 
+        sizes = keep.tile([P, ROW_PASSES, 2, N], F32, name="sizes", align_bytes=64)
+        for g in range(ROW_PASSES):
+            for e in range(2):
+                col = g * PACK + 2 + e
+                nc.scalar.activation(sizes[:, g, e, :], ts_bank[:], ACT.Copy, scale=negated[:, col : col + 1])
+
         def cast_x(g, shares):
-            grouped = keep.tile([P, K_PASS * PACK], BF16, name="x_by_d%d" % g, tag="x_by_d%d" % g, align_bytes=64)
-            dealt = grouped[:].rearrange("p (t m j) -> p m j t", t=PACK, j=PACK)
+            grouped = signed_rows[g][:, 2 * N :].bitcast(BF16)
+            dealt = grouped.rearrange("p (t m j) -> p m j t", t=PACK, j=PACK)
             source = x_raw[g][:].rearrange("p j (m t) -> p m j t", t=PACK)
             for copy, lo, hi in shares:
                 copy(dealt[:, lo:hi, :, :], source[:, lo:hi, :, :])
@@ -166,6 +175,10 @@ def tile_attend_gsig_wx_ts_kernel(tc, xT, wT, y, wt, ts, xm, offs, out_0, out_1)
                 nc.vector.scalar_tensor_tensor(
                     signed[g][:, t, :], signed[g][:, t, :], negated[:, col : col + 1], ts_bank[:], ALU.mult, ALU.mult
                 )
+
+        def factor_late(g):
+            for e in range(2):
+                nc.gpsimd.tensor_tensor(signed[g][:, 2 + e, :], late_signs[g][:, e, :], sizes[:, g, e, :], ALU.mult)
 
         def scores(g, x_d, banks):
             sig = keep.tile([P, PACK, N], F32, name="sig%d" % g, tag="sig%d" % g, align_bytes=64)
@@ -188,13 +201,13 @@ def tile_attend_gsig_wx_ts_kernel(tc, xT, wT, y, wt, ts, xm, offs, out_0, out_1)
             nc.vector.tensor_tensor(
                 grouped[:].rearrange("p (a s t) -> p s t a", a=PACK, t=PACK),
                 sig[:].rearrange("p t (s a) -> p s t a", a=PACK),
-                signed[g][:].rearrange("p t (s a) -> p s t a", a=PACK),
+                signed[g].rearrange("p t (s a) -> p s t a", a=PACK),
                 ALU.mult,
             )
             return grouped
 
-        def turn_h(g, grouped, banks):
-            turned = keep.tile([P, K_PASS * PACK], BF16, name="h_by_i%d" % g, tag="h_by_i%d" % g, align_bytes=64)
+        def turn_h(g, grouped, banks, slot):
+            turned = keep.tile([P, K_PASS * PACK], BF16, name="h_by_i%d" % g, tag=slot, align_bytes=64)
             view = turned[:].rearrange("s (u e p a) -> s u e p a", u=2, e=2, a=PACK)
             for u in range(2):
                 nc.scalar.copy(view[:, u, :, :, :], turn(grouped, u, banks[u]).rearrange("s a p e -> s e p a"))
@@ -209,11 +222,11 @@ def tile_attend_gsig_wx_ts_kernel(tc, xT, wT, y, wt, ts, xm, offs, out_0, out_1)
             out_view = out_1[0].rearrange("(g p t) d -> g p t d", p=P, t=PACK)[g]
             nc.scalar.dma_start(out_view[:, lo:hi, :], results[g][:, lo:hi, :])
 
-        def table_gradient(j, xm_r, b):
+        def table_gradient(j, xm_r, q, b, slot=""):
             bank = bank_tile(b, [P, N])
-            multiply(bank, xm_r, j % 2, h_r0, True, False)
-            multiply(bank, xm_r, 2 + j % 2, h_r1, False, True)
-            listed = keep.tile([P, N], F32, name="listed%d" % j)
+            multiply(bank, xm_r, q, h_r0, True, False)
+            multiply(bank, xm_r, 2 + q, h_r1, False, True)
+            listed = keep.tile([P, N], F32, name="listed%d" % j, tag=slot, align_bytes=64)
             nc.scalar.copy(listed[:].rearrange("p (s a) -> p s a", a=PACK), bank[:].rearrange("p (a s) -> p s a", a=PACK))
             return listed
 
@@ -227,29 +240,31 @@ def tile_attend_gsig_wx_ts_kernel(tc, xT, wT, y, wt, ts, xm, offs, out_0, out_1)
         w_view = w_by_i[:].rearrange("s (p u e a) -> s u p e a", u=2, e=2, a=PACK)
         for u in range(2):
             nc.scalar.copy(w_view[:, u, :, :, :], turn(w_by_d, u, 4 + u).rearrange("s a p e -> s p e a"))
-        x_grouped1 = cast_x(1, ((nc.scalar.copy, 0, P),))
-        factor(0, range(2))
         x_d0 = quantise("x_d0", x_grouped0, E4M3)
-        factor(0, range(2, PACK))
+        factor(0, range(2))
+        factor_late(0)
+        x_grouped1 = cast_x(1, ((nc.scalar.copy, X1_VECTOR, P),))
         sig0 = scores(0, x_d0, (0, 1, 2, 3))
-        factor(1, range(2))
+        cast_x(1, ((nc.vector.tensor_copy, 0, X1_VECTOR),))
+        factor(1, range(1))
         x_d1 = quantise("x_d1", x_grouped1, E4M3)
-        factor(1, range(2, PACK))
-        xm_low = keep.tile([P, D * PACK], BF16, name="xm_low", tag="logits0", align_bytes=64)
-        cast_xm(xm_low[:, : 2 * D], 0, 0)
+        factor(1, range(1, 2))
+        factor_late(1)
         sig1 = scores(1, x_d1, (4, 5, 6, 0))
         h0 = gradient(0, sig0)
+        xm_low = keep.tile([P, D * PACK], BF16, name="xm_low", tag="logits1", align_bytes=64)
+        cast_xm(xm_low[:, : 2 * D], 0, 0)
         cast_xm(xm_low[:, 2 * D :], 1, 0)
-        turned0 = turn_h(0, h0, (1, 2))
+        turned0 = turn_h(0, h0, (1, 2), "h_by_i0")
         h1 = gradient(1, sig1)
-        h_r0 = quantise("h_r0", h0, E5M2)
+        h_r0 = quantise("h_r0", h0, E5M2, slot="sig1")
         xm_r_low = quantise("xm_r_low", xm_low, E4M3)
         h_r1 = quantise("h_r1", h1, E5M2)
-        xm_high = keep.tile([P, D * PACK], BF16, name="xm_high", tag="logits1", align_bytes=64)
+        xm_high = keep.tile([P, D * PACK], BF16, name="xm_high", tag="logits0", align_bytes=64)
         cast_xm(xm_high[:, : 2 * D], 0, 1)
         cast_xm(xm_high[:, 2 * D :], 1, 1)
-        listed0 = table_gradient(0, xm_r_low, 3)
-        w_i = quantise("w_i", w_by_i, E4M3, slot="sig1")
+        listed0 = table_gradient(0, xm_r_low, 0, 3)
+        w_i = quantise("w_i", w_by_i, E4M3, slot="logits1")
         h_i0 = quantise("h_i0", turned0, E5M2, parts=2)
         xm_r_high = quantise("xm_r_high", xm_high, E4M3)
         results = [keep.tile([P, PACK, D], F32, name="rows%d" % g, tag="plane%d" % g, align_bytes=64) for g in range(ROW_PASSES)]
@@ -257,14 +272,14 @@ def tile_attend_gsig_wx_ts_kernel(tc, xT, wT, y, wt, ts, xm, offs, out_0, out_1)
             rows_gradient(0, h_i0, w_i, t, b)
             if t > 0:
                 store_rows(0, t - 1, t)
-        listed1 = table_gradient(1, xm_r_low, 4)
+        listed1 = table_gradient(1, xm_r_low, 1, 4)
         store_rows(0, PACK - 1, PACK)
         scatter(0, listed0)
-        turned1 = turn_h(1, h1, (3, 5))
+        turned1 = turn_h(1, h1, (3, 5), "h_by_i1")
         scatter(1, listed1)
         h_i1 = quantise("h_i1", turned1, E5M2)
-        listed2 = table_gradient(2, xm_r_high, 3)
-        listed3 = table_gradient(3, xm_r_high, 5)
+        listed2 = table_gradient(2, xm_r_high, 0, 3)
+        listed3 = table_gradient(3, xm_r_high, 1, 5)
         for t, b in enumerate((1, 2, 6, 0)):
             rows_gradient(1, h_i1, w_i, t, b)
             if t % 2 == 1:

@@ -67,11 +67,11 @@ def tile_attend_gsig_wx_ts_kernel(tc, xT, wT, y, wt, ts, xm, offs, out_0, out_1)
             return bank[:].rearrange("s a p -> s (a p)").bitcast(BF16).rearrange("s (a p e) -> s a p e", a=PACK, e=2)
 
         offsets = keep.tile([P, N // 16], U16, name="offsets")
-        nc.sync.dma_start(offsets[:], offs)
         ts_row = keep.tile([P, T], F32, name="ts_row")
         nc.gpsimd.memset(ts_row[:].bitcast(I32), 0)
-        weights = keep.tile([P, ROW_PASSES, PACK], F32, name="weights")
-        nc.scalar.dma_start(weights[:], wt[0].rearrange("(g p t) o -> p g (t o)", p=P, t=PACK))
+        padded = keep.tile([P, ROW_PASSES, 2 * PACK], F32, name="weights")
+        weights = padded[:, :, :PACK]
+        nc.scalar.dma_start(weights, wt[0].rearrange("(g p t) o -> p g (t o)", p=P, t=PACK))
         x_view = xT[0].rearrange("(p j) r -> p j r", j=PACK)
         y_view = y[0].rearrange("(g p t) i -> g p t i", p=P, t=PACK)
         xm_view = xm[0].rearrange("(g p t) d -> g p t d", p=P, t=PACK)
@@ -98,6 +98,7 @@ def tile_attend_gsig_wx_ts_kernel(tc, xT, wT, y, wt, ts, xm, offs, out_0, out_1)
             nc.sync.dma_start(plane[:], wT.rearrange("(p j) c -> p j c", j=PACK)[:, j, :])
             w_planes.append(plane)
             if j == 0:
+                nc.sync.dma_start(offsets[:], offs)
                 nc.sync.dma_start(ts_row[0:1, :], ts[0:1, :])
         x_raw = [load_x(0)]
         signed_rows = [keep.tile([P, PACK * N], F32, name="signed%d" % g, align_bytes=64) for g in range(ROW_PASSES)]
@@ -124,9 +125,8 @@ def tile_attend_gsig_wx_ts_kernel(tc, xT, wT, y, wt, ts, xm, offs, out_0, out_1)
         negated = keep.tile([P, ROW_PASSES * PACK], F32, name="negated")
         guarded = keep.tile([P, ROW_PASSES * PACK], F32, name="guarded")
         inverse = keep.tile([P, ROW_PASSES * PACK], F32, name="inverse")
-        flat = weights[:].rearrange("p g t -> p (g t)")
-        nc.vector.tensor_scalar(negated[:], flat, -1.0, None, ALU.mult)
-        nc.vector.scalar_tensor_tensor(guarded[:], flat, 0.0, flat, ALU.is_equal, ALU.add)
+        nc.vector.tensor_scalar(negated[:].rearrange("p (g t) -> p g t", t=PACK), weights, -1.0, None, ALU.mult)
+        nc.vector.scalar_tensor_tensor(guarded[:].rearrange("p (g t) -> p g t", t=PACK), weights, 0.0, weights, ALU.is_equal, ALU.add)
         nc.vector.reciprocal(inverse[:], guarded[:])
 
         w_by_d = keep.tile([P, N * PACK], BF16, name="w_by_d", align_bytes=64)

@@ -68,10 +68,11 @@ def tile_attend_gsig_wx_ts_kernel(tc, xT, wT, y, wt, ts, xm, offs, out_0, out_1)
 
         offsets = keep.tile([P, N // 16], U16, name="offsets")
         ts_row = keep.tile([P, T], F32, name="ts_row")
-        nc.gpsimd.memset(ts_row[:].bitcast(I32), 0)
+        nc.vector.memset(ts_row[:].bitcast(I32), 0)
         padded = keep.tile([P, ROW_PASSES, 2 * PACK], F32, name="weights")
         weights = padded[:, :, :PACK]
         nc.scalar.dma_start(weights, wt[0].rearrange("(g p t) o -> p g (t o)", p=P, t=PACK))
+        nc.scalar.dma_start(ts_row[0:1, :], ts[0:1, :])
         x_view = xT[0].rearrange("(p j) r -> p j r", j=PACK)
         y_view = y[0].rearrange("(g p t) i -> g p t i", p=P, t=PACK)
         xm_view = xm[0].rearrange("(g p t) d -> g p t d", p=P, t=PACK)
@@ -99,7 +100,6 @@ def tile_attend_gsig_wx_ts_kernel(tc, xT, wT, y, wt, ts, xm, offs, out_0, out_1)
             w_planes.append(plane)
             if j == 0:
                 nc.sync.dma_start(offsets[:], offs)
-                nc.sync.dma_start(ts_row[0:1, :], ts[0:1, :])
         x_raw = [load_x(0)]
         signed_rows = [keep.tile([P, PACK * N], F32, name="signed%d" % g, align_bytes=64) for g in range(ROW_PASSES)]
         signed = [rows[:].rearrange("p (t i) -> p t i", t=PACK) for rows in signed_rows]
@@ -114,13 +114,13 @@ def tile_attend_gsig_wx_ts_kernel(tc, xT, wT, y, wt, ts, xm, offs, out_0, out_1)
         nc.scalar.activation(warm[:], identity[:, 0:1], ACT.Sigmoid)
         windows = []
 
-        def clear_window():
-            window = keep.tile([P, T], F32, name="window%d" % len(windows))
-            nc.vector.memset(window[:].bitcast(I32), 0)
+        def clear_window(engine, slot):
+            window = keep.tile([P, T], F32, name="window%d" % len(windows), tag=slot, align_bytes=64)
+            engine.memset(window[:].bitcast(I32), 0)
             windows.append(window)
 
-        for count in range(3):
-            clear_window()
+        clear_window(nc.vector, "window0")
+        clear_window(nc.vector, "window1")
 
         negated = keep.tile([P, ROW_PASSES * PACK], F32, name="negated")
         guarded = keep.tile([P, ROW_PASSES * PACK], F32, name="guarded")
@@ -150,7 +150,7 @@ def tile_attend_gsig_wx_ts_kernel(tc, xT, wT, y, wt, ts, xm, offs, out_0, out_1)
         for c in range(PACK):
             nc.tensor.transpose(ts_bank[:, c * P : (c + 1) * P], ts_down[:, c : c + 1].to_broadcast([P, P]), identity[:])
 
-        sizes = keep.tile([P, ROW_PASSES, 2, N], F32, name="sizes", align_bytes=64)
+        sizes = keep.tile([P, ROW_PASSES, 2, N], F32, name="sizes", tag="sizes", align_bytes=64)
         for g in range(ROW_PASSES):
             for e in range(2):
                 col = g * PACK + 2 + e
@@ -250,6 +250,7 @@ def tile_attend_gsig_wx_ts_kernel(tc, xT, wT, y, wt, ts, xm, offs, out_0, out_1)
         x_d1 = quantise("x_d1", x_grouped1, E4M3)
         factor(1, range(1, 2))
         factor_late(1)
+        clear_window(nc.gpsimd, "sizes")
         sig1 = scores(1, x_d1, (4, 5, 6, 0))
         h0 = gradient(0, sig0)
         xm_low = keep.tile([P, D * PACK], BF16, name="xm_low", tag="logits1", align_bytes=64)

@@ -24,6 +24,7 @@ K_PASS = P * PACK
 ROW_PASSES = R // K_PASS
 X0_VECTOR = 80
 X1_VECTOR = 48
+ROOMS = {"turned": 0, "listed_vector": 4096, "listed_scalar": 6144}
 
 
 def tile_attend_gsig_wx_ts_kernel(tc, xT, wT, y, wt, ts, xm, offs, out_0, out_1):
@@ -32,11 +33,22 @@ def tile_attend_gsig_wx_ts_kernel(tc, xT, wT, y, wt, ts, xm, offs, out_0, out_1)
         keep = ctx.enter_context(tc.tile_pool(name="keep", bufs=1))
         psum = ctx.enter_context(tc.psum_pool(name="psum", bufs=1))
 
-        def bank_tile(b, shape):
-            return psum.tile(shape, F32, name="bank%d" % b)
+        shared = ctx.enter_context(tc.tile_pool(name="shared", bufs=1))
+        banks = [psum.tile([P, N], F32, name="bank%d" % b) for b in range(8)]
 
-        def quantise(name, grouped, fmt, slot="", parts=1, words=K_PASS):
-            codes = keep.tile([P, words], U32, name=name + "_codes", tag=slot, align_bytes=64)
+        def bank_tile(b, shape):
+            if len(shape) == 2:
+                return banks[b]
+            return banks[b][:, : shape[1] * shape[2]].rearrange("p (a c) -> p a c", a=shape[1])
+
+        def tenant(name, shape, dtype, room):
+            return shared.tile(shape, dtype, name=name, align_bytes=64, offset=ROOMS[room])
+
+        def quantise(name, grouped, fmt, slot="", parts=1, words=K_PASS, room=None):
+            if room is None:
+                codes = keep.tile([P, words], U32, name=name + "_codes", tag=slot, align_bytes=64)
+            else:
+                codes = tenant(name + "_codes", [P, words], U32, room)
             scales = keep.tile([P, words], U8, name=name + "_scales", align_bytes=64)
             width = words // parts
             for lo in range(0, words, width):
@@ -64,7 +76,7 @@ def tile_attend_gsig_wx_ts_kernel(tc, xT, wT, y, wt, ts, xm, offs, out_0, out_1)
             bank = bank_tile(b, [P, PACK, P])
             for a in range(PACK):
                 nc.tensor.transpose(bank[:, a, :], words[:, 2 * P * a + u : 2 * P * (a + 1) : 2], identity[:])
-            return bank[:].rearrange("s a p -> s (a p)").bitcast(BF16).rearrange("s (a p e) -> s a p e", a=PACK, e=2)
+            return banks[b][:].bitcast(BF16).rearrange("s (a p e) -> s a p e", a=PACK, e=2)
 
         offsets = keep.tile([P, N // 16], U16, name="offsets")
         ts_row = keep.tile([P, T], F32, name="ts_row")
@@ -84,7 +96,7 @@ def tile_attend_gsig_wx_ts_kernel(tc, xT, wT, y, wt, ts, xm, offs, out_0, out_1)
 
         def load_y(g):
             nc.sync.dma_start(signed[g][:, 0:2, :], y_view[g][:, 0:2, :])
-            late = keep.tile([P, 2, N], F32, name="late_signs%d" % g, align_bytes=64)
+            late = keep.tile([P, 2, N], F32, name="late_signs%d" % g, tag="late%d" % g, align_bytes=64)
             nc.sync.dma_start(late[:], y_view[g][:, 2:PACK, :])
             return late
 
@@ -135,8 +147,7 @@ def tile_attend_gsig_wx_ts_kernel(tc, xT, wT, y, wt, ts, xm, offs, out_0, out_1)
             nc.vector.tensor_copy(
                 w_by_d[:].rearrange("p (a s j) -> p s a j", a=PACK, j=PACK)[:, :, :, j], w_planes[j][:].indirect(offsets[:])
             )
-            if j == 0:
-                nc.vector.tensor_copy(ts_listed[:], ts_row[:].indirect(offsets[:]))
+        nc.scalar.activation(ts_listed[:], ts_row[:].indirect(offsets[:]), ACT.Copy)
         w_d = quantise("w_d", w_by_d, E4M3)
 
         ts_down = keep.tile([P, PACK], F32, name="ts_down")
@@ -164,10 +175,15 @@ def tile_attend_gsig_wx_ts_kernel(tc, xT, wT, y, wt, ts, xm, offs, out_0, out_1)
                 copy(dealt[:, lo:hi, :, :], source[:, lo:hi, :, :])
             return grouped
 
-        def cast_xm(grouped, g, half):
+        def cast_xm_low(grouped, g):
             woven = grouped.rearrange("p (c e t) -> p c t e", e=PACK, t=PACK)
-            source = xm_raw[g][:, :, half * D // 2 : (half + 1) * D // 2].rearrange("p t (c e) -> p c t e", e=PACK)
+            source = xm_raw[g][:, :, : D // 2].rearrange("p t (c e) -> p c t e", e=PACK)
             nc.scalar.copy(woven, source)
+
+        def cast_xm_high(grouped, g):
+            woven = grouped.rearrange("p (d t) -> p d t", t=PACK)
+            source = xm_raw[g][:, :, D // 2 :].rearrange("p t d -> p d t")
+            nc.gpsimd.tensor_scalar(woven, source, 1.0, 0.0, ALU.mult, ALU.add)
 
         def factor(g, places):
             for t in places:
@@ -180,12 +196,12 @@ def tile_attend_gsig_wx_ts_kernel(tc, xT, wT, y, wt, ts, xm, offs, out_0, out_1)
             for e in range(2):
                 nc.gpsimd.tensor_tensor(signed[g][:, 2 + e, :], late_signs[g][:, e, :], sizes[:, g, e, :], ALU.mult)
 
-        def scores(g, x_d, banks):
+        def scores(g, x_d, picked):
             sig = keep.tile([P, PACK, N], F32, name="sig%d" % g, tag="sig%d" % g, align_bytes=64)
             logits = keep.tile([P, PACK, N], F32, name="logits%d" % g, tag="logits%d" % g, align_bytes=64)
             for t in range(PACK):
                 col = g * PACK + t
-                bank = bank_tile(banks[t], [P, N])
+                bank = bank_tile(picked[t], [P, N])
                 multiply(bank, x_d, t, w_d, True, True)
                 nc.vector.tensor_tensor(
                     logits[:, t, :].rearrange("p (s a) -> p s a", a=PACK),
@@ -198,42 +214,46 @@ def tile_attend_gsig_wx_ts_kernel(tc, xT, wT, y, wt, ts, xm, offs, out_0, out_1)
 
         def gradient(g, sig):
             grouped = keep.tile([P, N * PACK], BF16, name="h_by_r%d" % g, align_bytes=64)
-            nc.vector.tensor_tensor(
-                grouped[:].rearrange("p (a s t) -> p s t a", a=PACK, t=PACK),
-                sig[:].rearrange("p t (s a) -> p s t a", a=PACK),
-                signed[g].rearrange("p t (s a) -> p s t a", a=PACK),
-                ALU.mult,
-            )
+            for lo in (0, 2):
+                nc.vector.tensor_tensor(
+                    grouped[:].rearrange("p (a s t) -> p s t a", a=PACK, t=PACK)[:, :, :, lo : lo + 2],
+                    sig[:].rearrange("p t (s a) -> p s t a", a=PACK)[:, :, :, lo : lo + 2],
+                    signed[g].rearrange("p t (s a) -> p s t a", a=PACK)[:, :, :, lo : lo + 2],
+                    ALU.mult,
+                )
             return grouped
 
-        def turn_h(g, grouped, banks, slot):
-            turned = keep.tile([P, K_PASS * PACK], BF16, name="h_by_i%d" % g, tag=slot, align_bytes=64)
-            view = turned[:].rearrange("s (u e p a) -> s u e p a", u=2, e=2, a=PACK)
-            for u in range(2):
-                nc.scalar.copy(view[:, u, :, :, :], turn(grouped, u, banks[u]).rearrange("s a p e -> s e p a"))
-            return turned
+        def turn_h(turned, grouped, u, b):
+            view = turned.rearrange("s (e p a) -> s e p a", e=2, a=PACK)
+            nc.scalar.copy(view, turn(grouped, u, b).rearrange("s a p e -> s e p a"))
 
-        def rows_gradient(g, h_i, w_i, t, b):
+        def rows_gradient(copy, result, h_i, q, w_i, b):
             bank = bank_tile(b, [P, D])
-            multiply(bank, h_i, t, w_i, True, True)
-            nc.scalar.copy(results[g][:, t, :], bank[:])
+            multiply(bank, h_i, q, w_i, True, True)
+            copy(result, bank[:])
 
-        def store_rows(g, lo, hi):
+        def store_rows(engine, g, lo, hi, result):
             out_view = out_1[0].rearrange("(g p t) d -> g p t d", p=P, t=PACK)[g]
-            nc.scalar.dma_start(out_view[:, lo:hi, :], results[g][:, lo:hi, :])
+            engine.dma_start(out_view[:, lo:hi, :], result)
 
-        def table_gradient(j, xm_r, q, b, slot=""):
+        def table_gradient(copy, j, xm_r, q, b, slot):
             bank = bank_tile(b, [P, N])
             multiply(bank, xm_r, q, h_r0, True, False)
             multiply(bank, xm_r, 2 + q, h_r1, False, True)
-            listed = keep.tile([P, N], F32, name="listed%d" % j, tag=slot, align_bytes=64)
-            nc.scalar.copy(listed[:].rearrange("p (s a) -> p s a", a=PACK), bank[:].rearrange("p (a s) -> p s a", a=PACK))
+            listed = tenant("listed%d" % j, [P, N], F32, slot)
+            copy(listed[:].rearrange("p (s a) -> p s a", a=PACK), bank[:].rearrange("p (a s) -> p s a", a=PACK))
             return listed
 
-        def scatter(j, listed):
-            window = windows[j % len(windows)]
-            nc.vector.tensor_copy(window[:].indirect(offsets[:]), listed[:])
-            nc.sync.dma_start(out_0[j * P : (j + 1) * P, :], window[:])
+        def scatter_vector(j, listed):
+            nc.vector.tensor_copy(windows[j][:].indirect(offsets[:]), listed[:])
+
+        def scatter_scalar(j, listed):
+            for half in range(2):
+                part = offsets[:, half * N // 32 : (half + 1) * N // 32]
+                nc.scalar.activation(windows[j][:].indirect(part), listed[:, half * N // 2 : (half + 1) * N // 2], ACT.Copy)
+
+        def store_window(engine, j):
+            engine.dma_start(out_0[j * P : (j + 1) * P, :], windows[j][:])
 
         x_grouped0 = cast_x(0, ((nc.vector.tensor_copy, 0, X0_VECTOR), (nc.scalar.copy, X0_VECTOR, P)))
         w_by_i = keep.tile([P, D * PACK], BF16, name="w_by_i", tag="w_by_i", align_bytes=64)
@@ -251,39 +271,57 @@ def tile_attend_gsig_wx_ts_kernel(tc, xT, wT, y, wt, ts, xm, offs, out_0, out_1)
         factor(1, range(1, 2))
         factor_late(1)
         clear_window(nc.gpsimd, "sizes")
+        clear_window(nc.gpsimd, "late1")
+        xm_low = keep.tile([P, D * PACK], BF16, name="xm_low", tag="logits0", align_bytes=64)
+        cast_xm_low(xm_low[:, : 2 * D], 0)
         sig1 = scores(1, x_d1, (4, 5, 6, 0))
         h0 = gradient(0, sig0)
-        xm_low = keep.tile([P, D * PACK], BF16, name="xm_low", tag="logits1", align_bytes=64)
-        cast_xm(xm_low[:, : 2 * D], 0, 0)
-        cast_xm(xm_low[:, 2 * D :], 1, 0)
-        turned0 = turn_h(0, h0, (1, 2), "h_by_i0")
+        cast_xm_low(xm_low[:, 2 * D :], 1)
+        half = 2 * K_PASS
+        turned0 = tenant("h_by_i0", [P, 2 * half], BF16, "turned")
+        for u in range(2):
+            turn_h(turned0[:, u * half : (u + 1) * half], h0, u, 1 + u)
         h1 = gradient(1, sig1)
+        turned1 = [keep.tile([P, half], BF16, name="h_by_i1_%d" % u, align_bytes=64) for u in range(2)]
+        turn_h(turned1[0][:], h1, 0, 3)
+        turn_h(turned1[1][:], h1, 1, 7)
         h_r0 = quantise("h_r0", h0, E5M2, slot="sig1")
         xm_r_low = quantise("xm_r_low", xm_low, E4M3)
         h_r1 = quantise("h_r1", h1, E5M2)
-        xm_high = keep.tile([P, D * PACK], BF16, name="xm_high", tag="logits0", align_bytes=64)
-        cast_xm(xm_high[:, : 2 * D], 0, 1)
-        cast_xm(xm_high[:, 2 * D :], 1, 1)
-        listed0 = table_gradient(0, xm_r_low, 0, 3)
-        w_i = quantise("w_i", w_by_i, E4M3, slot="logits1")
-        h_i0 = quantise("h_i0", turned0, E5M2, parts=2)
+        listed0 = table_gradient(nc.scalar.copy, 0, xm_r_low, 0, 4, "listed_vector")
+        w_i = quantise("w_i", w_by_i, E4M3, slot="logits0")
+        h_i0a = quantise("h_i0a", turned0[:, :half], E5M2, words=2 * P)
+        h_i1a = quantise("h_i1a", turned1[0], E5M2, words=2 * P)
+        h_i1b = quantise("h_i1b", turned1[1], E5M2, words=2 * P)
+        h_i0b = quantise("h_i0b", turned0[:, half:], E5M2, words=2 * P)
+        scatter_vector(0, listed0)
+        store_window(nc.sync, 0)
+        xm_high = tenant("xm_high", [P, D * PACK], BF16, "turned")
+        cast_xm_high(xm_high[:, : 2 * D], 0)
+        cast_xm_high(xm_high[:, 2 * D :], 1)
+        rows0 = keep.tile([P, PACK, D], F32, name="rows0", tag="plane0", align_bytes=64)
+        rows1a = keep.tile([P, 1, D], F32, name="rows1a", tag="plane1", align_bytes=64)
+        for t, b in enumerate((5, 6, 0, 1)):
+            rows_gradient(nc.scalar.copy, rows0[:, t, :], h_i0b if t >= 2 else h_i0a, t % 2, w_i, b)
+            if t in (1, 2):
+                store_rows(nc.scalar, 0, t - 1, t, rows0[:, t - 1 : t, :])
+        rows_gradient(nc.scalar.copy, rows1a[:, 0, :], h_i1a, 0, w_i, 2)
+        store_rows(nc.scalar, 0, 2, PACK, rows0[:, 2:, :])
+        listed1 = table_gradient(nc.scalar.copy, 1, xm_r_low, 1, 6, "listed_scalar")
+        store_rows(nc.scalar, 1, 0, 1, rows1a[:])
+        scatter_scalar(1, listed1)
         xm_r_high = quantise("xm_r_high", xm_high, E4M3)
-        results = [keep.tile([P, PACK, D], F32, name="rows%d" % g, tag="plane%d" % g, align_bytes=64) for g in range(ROW_PASSES)]
-        for t, b in enumerate((4, 5, 6, 0)):
-            rows_gradient(0, h_i0, w_i, t, b)
-            if t > 0:
-                store_rows(0, t - 1, t)
-        listed1 = table_gradient(1, xm_r_low, 1, 4)
-        store_rows(0, PACK - 1, PACK)
-        scatter(0, listed0)
-        turned1 = turn_h(1, h1, (3, 5), "h_by_i1")
-        scatter(1, listed1)
-        h_i1 = quantise("h_i1", turned1, E5M2)
-        listed2 = table_gradient(2, xm_r_high, 0, 3)
-        listed3 = table_gradient(3, xm_r_high, 1, 5)
-        for t, b in enumerate((1, 2, 6, 0)):
-            rows_gradient(1, h_i1, w_i, t, b)
-            if t % 2 == 1:
-                store_rows(1, t - 1, t + 1)
-        scatter(2, listed2)
-        scatter(3, listed3)
+        rows1b = tenant("rows1b", [P, 2, D], F32, "turned")
+        rows_gradient(nc.vector.tensor_copy, rows1b[:, 0, :], h_i1a, 1, w_i, 3)
+        rows_gradient(nc.vector.tensor_copy, rows1b[:, 1, :], h_i1b, 0, w_i, 7)
+        store_rows(nc.sync, 1, 1, 3, rows1b[:])
+        listed2 = table_gradient(nc.vector.tensor_copy, 2, xm_r_high, 0, 0, "listed_vector")
+        scatter_vector(2, listed2)
+        store_window(nc.sync, 2)
+        rows1c = tenant("rows1c", [P, 1, D], F32, "listed_vector")
+        rows_gradient(nc.vector.tensor_copy, rows1c[:, 0, :], h_i1b, 1, w_i, 4)
+        store_rows(nc.sync, 1, 3, PACK, rows1c[:])
+        listed3 = table_gradient(nc.scalar.copy, 3, xm_r_high, 1, 1, "listed_scalar")
+        store_window(nc.scalar, 1)
+        scatter_scalar(3, listed3)
+        store_window(nc.scalar, 3)

@@ -24,6 +24,7 @@ K_PASS = P * PACK
 ROW_PASSES = R // K_PASS
 X0_VECTOR = 80
 X1_VECTOR = 48
+EARLY_SLOTS = 256
 ROOMS = {"turned": 0, "listed_vector": 4096, "listed_scalar": 6144}
 
 
@@ -80,11 +81,11 @@ def tile_attend_gsig_wx_ts_kernel(tc, xT, wT, y, wt, ts, xm, offs, out_0, out_1)
 
         offsets = keep.tile([P, N // 16], U16, name="offsets")
         ts_row = keep.tile([P, T], F32, name="ts_row")
-        nc.vector.memset(ts_row[:].bitcast(I32), 0)
+        nc.vector.memset(ts_row[0 : P - 1, :].bitcast(I32), 0)
         padded = keep.tile([P, ROW_PASSES, 2 * PACK], F32, name="weights")
         weights = padded[:, :, :PACK]
         nc.scalar.dma_start(weights, wt[0].rearrange("(g p t) o -> p g (t o)", p=P, t=PACK))
-        nc.scalar.dma_start(ts_row[0:1, :], ts[0:1, :])
+        nc.scalar.dma_start(ts_row[P - 1 : P, :], ts[0:1, :])
         x_view = xT[0].rearrange("(p j) r -> p j r", j=PACK)
         y_view = y[0].rearrange("(g p t) i -> g p t i", p=P, t=PACK)
         xm_view = xm[0].rearrange("(g p t) d -> g p t d", p=P, t=PACK)
@@ -123,7 +124,7 @@ def tile_attend_gsig_wx_ts_kernel(tc, xT, wT, y, wt, ts, xm, offs, out_0, out_1)
         identity = keep.tile([P, P], F32, name="identity")
         make_identity(nc, identity[:])
         warm = keep.tile([P, 1], F32, name="warm")
-        nc.scalar.activation(warm[:], identity[:, 0:1], ACT.Sigmoid)
+        nc.scalar.activation(warm[:], padded[:, 0, 0:1], ACT.Sigmoid)
         windows = []
 
         def clear_window(engine, slot):
@@ -156,7 +157,7 @@ def tile_attend_gsig_wx_ts_kernel(tc, xT, wT, y, wt, ts, xm, offs, out_0, out_1)
             for c in range(2):
                 block = 2 * half + c
                 nc.tensor.transpose(bank[:, c, :], ts_listed[:, block * P : (block + 1) * P], identity[:])
-            nc.scalar.copy(ts_down[:, 2 * half : 2 * half + 2], bank[:, :, 0])
+            nc.scalar.copy(ts_down[:, 2 * half : 2 * half + 2], bank[:, :, P - 1])
         ts_bank = bank_tile(7, [P, N])
         for c in range(PACK):
             nc.tensor.transpose(ts_bank[:, c * P : (c + 1) * P], ts_down[:, c : c + 1].to_broadcast([P, P]), identity[:])
@@ -236,16 +237,20 @@ def tile_attend_gsig_wx_ts_kernel(tc, xT, wT, y, wt, ts, xm, offs, out_0, out_1)
             out_view = out_1[0].rearrange("(g p t) d -> g p t d", p=P, t=PACK)[g]
             engine.dma_start(out_view[:, lo:hi, :], result)
 
-        def table_gradient(copy, j, xm_r, q, b, slot):
+        def unload(copy, listed, b, lo, hi):
+            ordered = listed[:].rearrange("p (s a) -> p s a", a=PACK)
+            copy(ordered[:, lo:hi, :], banks[b][:].rearrange("p (a s) -> p s a", a=PACK)[:, lo:hi, :])
+
+        def table_gradient(copy, j, xm_r, q, b, slot, groups=P):
             bank = bank_tile(b, [P, N])
             multiply(bank, xm_r, q, h_r0, True, False)
             multiply(bank, xm_r, 2 + q, h_r1, False, True)
             listed = tenant("listed%d" % j, [P, N], F32, slot)
-            copy(listed[:].rearrange("p (s a) -> p s a", a=PACK), bank[:].rearrange("p (a s) -> p s a", a=PACK))
+            unload(copy, listed, b, 0, groups)
             return listed
 
-        def scatter_vector(j, listed):
-            nc.vector.tensor_copy(windows[j][:].indirect(offsets[:]), listed[:])
+        def scatter_vector(j, listed, lo=0, hi=N):
+            nc.vector.tensor_copy(windows[j][:].indirect(offsets[:, lo // 16 : hi // 16]), listed[:, lo:hi])
 
         def scatter_scalar(j, listed):
             for half in range(2):
@@ -288,14 +293,13 @@ def tile_attend_gsig_wx_ts_kernel(tc, xT, wT, y, wt, ts, xm, offs, out_0, out_1)
         h_r0 = quantise("h_r0", h0, E5M2, slot="sig1")
         xm_r_low = quantise("xm_r_low", xm_low, E4M3)
         h_r1 = quantise("h_r1", h1, E5M2)
-        listed0 = table_gradient(nc.scalar.copy, 0, xm_r_low, 0, 4, "listed_vector")
+        listed0 = table_gradient(nc.scalar.copy, 0, xm_r_low, 0, 4, "listed_vector", EARLY_SLOTS // PACK)
         w_i = quantise("w_i", w_by_i, E4M3, slot="logits0")
         h_i0a = quantise("h_i0a", turned0[:, :half], E5M2, words=2 * P)
         h_i1a = quantise("h_i1a", turned1[0], E5M2, words=2 * P)
         h_i1b = quantise("h_i1b", turned1[1], E5M2, words=2 * P)
         h_i0b = quantise("h_i0b", turned0[:, half:], E5M2, words=2 * P)
-        scatter_vector(0, listed0)
-        store_window(nc.sync, 0)
+        scatter_vector(0, listed0, 0, EARLY_SLOTS)
         xm_high = tenant("xm_high", [P, D * PACK], BF16, "turned")
         cast_xm_high(xm_high[:, : 2 * D], 0)
         cast_xm_high(xm_high[:, 2 * D :], 1)
@@ -303,8 +307,12 @@ def tile_attend_gsig_wx_ts_kernel(tc, xT, wT, y, wt, ts, xm, offs, out_0, out_1)
         rows1a = keep.tile([P, 1, D], F32, name="rows1a", tag="plane1", align_bytes=64)
         for t, b in enumerate((5, 6, 0, 1)):
             rows_gradient(nc.scalar.copy, rows0[:, t, :], h_i0b if t >= 2 else h_i0a, t % 2, w_i, b)
-            if t in (1, 2):
-                store_rows(nc.scalar, 0, t - 1, t, rows0[:, t - 1 : t, :])
+            if t < 2:
+                store_rows(nc.sync, 0, t, t + 1, rows0[:, t : t + 1, :])
+            if t == 1:
+                unload(nc.scalar.copy, listed0, 4, EARLY_SLOTS // PACK, P)
+        scatter_vector(0, listed0, EARLY_SLOTS, N)
+        store_window(nc.sync, 0)
         rows_gradient(nc.scalar.copy, rows1a[:, 0, :], h_i1a, 0, w_i, 2)
         store_rows(nc.scalar, 0, 2, PACK, rows0[:, 2:, :])
         listed1 = table_gradient(nc.scalar.copy, 1, xm_r_low, 1, 6, "listed_scalar")

@@ -304,7 +304,7 @@ def tile_attend_gsig_wx_ts_kernel(tc, xT, wT, y, wt, ts, xm, offs, out_0, out_1)
         cast_xm_high(xm_high[:, : 2 * D], 0)
         cast_xm_high(xm_high[:, 2 * D :], 1)
         rows0 = keep.tile([P, PACK, D], F32, name="rows0", tag="plane0", align_bytes=64)
-        rows1a = keep.tile([P, 1, D], F32, name="rows1a", tag="plane1", align_bytes=64)
+        rows1a = keep.tile([P, 2, D], F32, name="rows1a", tag="plane1", align_bytes=64)
         for t, b in enumerate((5, 6, 0, 1)):
             rows_gradient(nc.scalar.copy, rows0[:, t, :], h_i0b if t >= 2 else h_i0a, t % 2, w_i, b)
             if t < 2:
@@ -315,20 +315,18 @@ def tile_attend_gsig_wx_ts_kernel(tc, xT, wT, y, wt, ts, xm, offs, out_0, out_1)
         store_window(nc.sync, 0)
         rows_gradient(nc.scalar.copy, rows1a[:, 0, :], h_i1a, 0, w_i, 2)
         store_rows(nc.scalar, 0, 2, PACK, rows0[:, 2:, :])
+        rows_gradient(nc.scalar.copy, rows1a[:, 1, :], h_i1a, 1, w_i, 3)
         listed1 = table_gradient(nc.scalar.copy, 1, xm_r_low, 1, 6, "listed_scalar")
-        store_rows(nc.scalar, 1, 0, 1, rows1a[:])
+        store_rows(nc.scalar, 1, 0, 2, rows1a[:])
         scatter_scalar(1, listed1)
         xm_r_high = quantise("xm_r_high", xm_high, E4M3)
         rows1b = tenant("rows1b", [P, 2, D], F32, "turned")
-        rows_gradient(nc.vector.tensor_copy, rows1b[:, 0, :], h_i1a, 1, w_i, 3)
-        rows_gradient(nc.vector.tensor_copy, rows1b[:, 1, :], h_i1b, 0, w_i, 7)
-        store_rows(nc.sync, 1, 1, 3, rows1b[:])
+        rows_gradient(nc.vector.tensor_copy, rows1b[:, 0, :], h_i1b, 0, w_i, 7)
+        rows_gradient(nc.vector.tensor_copy, rows1b[:, 1, :], h_i1b, 1, w_i, 5)
+        store_rows(nc.sync, 1, 2, PACK, rows1b[:])
         listed2 = table_gradient(nc.vector.tensor_copy, 2, xm_r_high, 0, 0, "listed_vector")
         scatter_vector(2, listed2)
         store_window(nc.sync, 2)
-        rows1c = tenant("rows1c", [P, 1, D], F32, "listed_vector")
-        rows_gradient(nc.vector.tensor_copy, rows1c[:, 0, :], h_i1b, 1, w_i, 4)
-        store_rows(nc.sync, 1, 3, PACK, rows1c[:])
         listed3 = table_gradient(nc.scalar.copy, 3, xm_r_high, 1, 1, "listed_scalar")
         store_window(nc.scalar, 1)
         scatter_scalar(3, listed3)

@@ -24,8 +24,7 @@ K_PASS = P * PACK
 ROW_PASSES = R // K_PASS
 X0_VECTOR = 80
 X1_VECTOR = 48
-EARLY_SLOTS = 256
-ROOMS = {"turned": 0, "listed_vector": 4096, "listed_scalar": 6144}
+ROOMS = {"turned": 0, "xm_late3": 5120, "xm_late2": 3072, "codes2": 11776, "codes3": 12800, "last_rows": 1024, "listed_late": 8192, "turned_last": 4096, "listed_vector": 12288, "listed_scalar": 16384}
 
 
 def tile_attend_gsig_wx_ts_kernel(tc, xT, wT, y, wt, ts, xm, offs, out_0, out_1):
@@ -181,10 +180,13 @@ def tile_attend_gsig_wx_ts_kernel(tc, xT, wT, y, wt, ts, xm, offs, out_0, out_1)
             source = xm_raw[g][:, :, : D // 2].rearrange("p t (c e) -> p c t e", e=PACK)
             nc.scalar.copy(woven, source)
 
-        def cast_xm_high(grouped, g):
-            woven = grouped.rearrange("p (d t) -> p d t", t=PACK)
-            source = xm_raw[g][:, :, D // 2 :].rearrange("p t d -> p d t")
-            nc.gpsimd.tensor_scalar(woven, source, 1.0, 0.0, ALU.mult, ALU.add)
+        def late_xm(j):
+            grouped = tenant("xm_late%d" % j, [P, ROW_PASSES * K_PASS], BF16, "xm_late%d" % j)
+            for g in range(ROW_PASSES):
+                woven = grouped[:, g * K_PASS : (g + 1) * K_PASS].rearrange("p (d t) -> p d t", t=PACK)
+                source = xm_raw[g][:, :, j * P : (j + 1) * P].rearrange("p t d -> p d t")
+                nc.gpsimd.tensor_scalar(woven, source, 1.0, 0.0, ALU.mult, ALU.add)
+            return grouped
 
         def factor(g, places):
             for t in places:
@@ -241,10 +243,10 @@ def tile_attend_gsig_wx_ts_kernel(tc, xT, wT, y, wt, ts, xm, offs, out_0, out_1)
             ordered = listed[:].rearrange("p (s a) -> p s a", a=PACK)
             copy(ordered[:, lo:hi, :], banks[b][:].rearrange("p (a s) -> p s a", a=PACK)[:, lo:hi, :])
 
-        def table_gradient(copy, j, xm_r, q, b, slot, groups=P):
+        def table_gradient(copy, j, xm_r, q, b, slot, groups=P, step=2):
             bank = bank_tile(b, [P, N])
             multiply(bank, xm_r, q, h_r0, True, False)
-            multiply(bank, xm_r, 2 + q, h_r1, False, True)
+            multiply(bank, xm_r, step + q, h_r1, False, True)
             listed = tenant("listed%d" % j, [P, N], F32, slot)
             unload(copy, listed, b, 0, groups)
             return listed
@@ -252,10 +254,9 @@ def tile_attend_gsig_wx_ts_kernel(tc, xT, wT, y, wt, ts, xm, offs, out_0, out_1)
         def scatter_vector(j, listed, lo=0, hi=N):
             nc.vector.tensor_copy(windows[j][:].indirect(offsets[:, lo // 16 : hi // 16]), listed[:, lo:hi])
 
-        def scatter_scalar(j, listed):
-            for half in range(2):
-                part = offsets[:, half * N // 32 : (half + 1) * N // 32]
-                nc.scalar.activation(windows[j][:].indirect(part), listed[:, half * N // 2 : (half + 1) * N // 2], ACT.Copy)
+        def scatter_scalar(j, listed, half):
+            part = offsets[:, half * N // 32 : (half + 1) * N // 32]
+            nc.scalar.activation(windows[j][:].indirect(part), listed[:, half * N // 2 : (half + 1) * N // 2], ACT.Copy)
 
         def store_window(engine, j):
             engine.dma_start(out_0[j * P : (j + 1) * P, :], windows[j][:])
@@ -287,47 +288,48 @@ def tile_attend_gsig_wx_ts_kernel(tc, xT, wT, y, wt, ts, xm, offs, out_0, out_1)
         for u in range(2):
             turn_h(turned0[:, u * half : (u + 1) * half], h0, u, 1 + u)
         h1 = gradient(1, sig1)
-        turned1 = [keep.tile([P, half], BF16, name="h_by_i1_%d" % u, align_bytes=64) for u in range(2)]
+        turned1 = [keep.tile([P, half], BF16, name="h_by_i1_0", align_bytes=64), tenant("h_by_i1_1", [P, half], BF16, "turned_last")]
         turn_h(turned1[0][:], h1, 0, 3)
         turn_h(turned1[1][:], h1, 1, 7)
         h_r0 = quantise("h_r0", h0, E5M2, slot="sig1")
         xm_r_low = quantise("xm_r_low", xm_low, E4M3)
         h_r1 = quantise("h_r1", h1, E5M2)
-        listed0 = table_gradient(nc.scalar.copy, 0, xm_r_low, 0, 4, "listed_vector", EARLY_SLOTS // PACK)
+        listed0 = table_gradient(nc.scalar.copy, 0, xm_r_low, 0, 4, "listed_vector")
         w_i = quantise("w_i", w_by_i, E4M3, slot="logits0")
         h_i0a = quantise("h_i0a", turned0[:, :half], E5M2, words=2 * P)
+        h_i0b = quantise("h_i0b", turned0[:, half:], E5M2, words=2 * P)
         h_i1a = quantise("h_i1a", turned1[0], E5M2, words=2 * P)
         h_i1b = quantise("h_i1b", turned1[1], E5M2, words=2 * P)
-        h_i0b = quantise("h_i0b", turned0[:, half:], E5M2, words=2 * P)
-        scatter_vector(0, listed0, 0, EARLY_SLOTS)
-        xm_high = tenant("xm_high", [P, D * PACK], BF16, "turned")
-        cast_xm_high(xm_high[:, : 2 * D], 0)
-        cast_xm_high(xm_high[:, 2 * D :], 1)
-        rows0 = keep.tile([P, PACK, D], F32, name="rows0", tag="plane0", align_bytes=64)
+        scatter_vector(0, listed0)
+        store_window(nc.sync, 0)
+        late = [late_xm(2), late_xm(3)]
         rows1a = keep.tile([P, 2, D], F32, name="rows1a", tag="plane1", align_bytes=64)
+        rows0 = keep.tile([P, PACK, D], F32, name="rows0", tag="plane0", align_bytes=64)
         for t, b in enumerate((5, 6, 0, 1)):
             rows_gradient(nc.scalar.copy, rows0[:, t, :], h_i0b if t >= 2 else h_i0a, t % 2, w_i, b)
-            if t < 2:
-                store_rows(nc.sync, 0, t, t + 1, rows0[:, t : t + 1, :])
-            if t == 1:
-                unload(nc.scalar.copy, listed0, 4, EARLY_SLOTS // PACK, P)
-        scatter_vector(0, listed0, EARLY_SLOTS, N)
-        store_window(nc.sync, 0)
+            if t in (1, 2):
+                store_rows(nc.scalar, 0, t - 1, t, rows0[:, t - 1 : t, :])
         rows_gradient(nc.scalar.copy, rows1a[:, 0, :], h_i1a, 0, w_i, 2)
         store_rows(nc.scalar, 0, 2, PACK, rows0[:, 2:, :])
+        listed1 = table_gradient(nc.scalar.copy, 1, xm_r_low, 1, 6, "listed_scalar", P // 2)
+        store_rows(nc.scalar, 1, 0, 1, rows1a[:, 0:1, :])
+        unload(nc.scalar.copy, listed1, 6, P // 2, P)
+        scatter_scalar(1, listed1, 0)
         rows_gradient(nc.scalar.copy, rows1a[:, 1, :], h_i1a, 1, w_i, 3)
-        listed1 = table_gradient(nc.scalar.copy, 1, xm_r_low, 1, 6, "listed_scalar")
-        store_rows(nc.scalar, 1, 0, 2, rows1a[:])
-        scatter_scalar(1, listed1)
-        xm_r_high = quantise("xm_r_high", xm_high, E4M3)
-        rows1b = tenant("rows1b", [P, 2, D], F32, "turned")
+        scatter_scalar(1, listed1, 1)
+        store_rows(nc.scalar, 1, 1, 2, rows1a[:, 1:2, :])
+        xm_r2 = quantise("xm_r2", late[0], E4M3, words=2 * P, room="codes2")
+        xm_r3 = quantise("xm_r3", late[1], E4M3, words=2 * P, room="codes3")
+        rows1b = tenant("rows1b", [P, 2, D], F32, "last_rows")
         rows_gradient(nc.vector.tensor_copy, rows1b[:, 0, :], h_i1b, 0, w_i, 7)
         rows_gradient(nc.vector.tensor_copy, rows1b[:, 1, :], h_i1b, 1, w_i, 5)
         store_rows(nc.sync, 1, 2, PACK, rows1b[:])
-        listed2 = table_gradient(nc.vector.tensor_copy, 2, xm_r_high, 0, 0, "listed_vector")
+        listed2 = table_gradient(nc.vector.tensor_copy, 2, xm_r2, 0, 0, "listed_late", step=1)
         scatter_vector(2, listed2)
         store_window(nc.sync, 2)
-        listed3 = table_gradient(nc.scalar.copy, 3, xm_r_high, 1, 1, "listed_scalar")
+        listed3 = table_gradient(nc.scalar.copy, 3, xm_r3, 0, 7, "listed_scalar", P // 2, step=1)
         store_window(nc.scalar, 1)
-        scatter_scalar(3, listed3)
+        unload(nc.scalar.copy, listed3, 7, P // 2, P)
+        for piece in range(2):
+            scatter_scalar(3, listed3, piece)
         store_window(nc.scalar, 3)

@@ -307,10 +307,10 @@ def tile_attend_gsig_wx_ts_kernel(tc, xT, wT, y, wt, ts, xm, offs, out_0, out_1)
         rows0 = keep.tile([P, PACK, D], F32, name="rows0", tag="plane0", align_bytes=64)
         for t, b in enumerate((5, 6, 0, 1)):
             rows_gradient(nc.scalar.copy, rows0[:, t, :], h_i0b if t >= 2 else h_i0a, t % 2, w_i, b)
-            if t in (1, 2):
+            if t:
                 store_rows(nc.scalar, 0, t - 1, t, rows0[:, t - 1 : t, :])
         rows_gradient(nc.scalar.copy, rows1a[:, 0, :], h_i1a, 0, w_i, 2)
-        store_rows(nc.scalar, 0, 2, PACK, rows0[:, 2:, :])
+        store_rows(nc.scalar, 0, 3, PACK, rows0[:, 3:, :])
         listed1 = table_gradient(nc.scalar.copy, 1, xm_r_low, 1, 6, "listed_scalar", P // 2)
         store_rows(nc.scalar, 1, 0, 1, rows1a[:, 0:1, :])
         unload(nc.scalar.copy, listed1, 6, P // 2, P)

from contextlib import ExitStack

import concourse.mybir as mybir
from concourse.masks import make_identity

N, T, D, R = 512, 2048, 512, 1024
FLOPS = 3 * 2 * N * D * R
BYTES = 4 * (2 * D * R + 2 * D * T + R * N + R + T + R * D) + 2 * 128 * (N // 16)

F32 = mybir.dt.float32
BF16 = mybir.dt.bfloat16
I32 = mybir.dt.int32
U32 = mybir.dt.uint32
U16 = mybir.dt.uint16
U8 = mybir.dt.uint8
E4M3 = mybir.dt.float8_e4m3fn_x4
E5M2 = mybir.dt.float8_e5m2_x4
ALU = mybir.AluOpType
ACT = mybir.ActivationFunctionType

P = 128
PACK = 4
K_PASS = P * PACK
ROW_PASSES = R // K_PASS
X0_VECTOR = 80
X1_VECTOR = 48
ROOMS = {"turned": 0, "xm_late3": 5120, "xm_late2": 3072, "codes2": 11776, "codes3": 12800, "last_rows": 1024, "listed_late": 8192, "turned_last": 4096, "listed_vector": 12288, "listed_scalar": 16384}


def tile_attend_gsig_wx_ts_kernel(tc, xT, wT, y, wt, ts, xm, offs, out_0, out_1):
    nc = tc.nc
    with ExitStack() as ctx:
        keep = ctx.enter_context(tc.tile_pool(name="keep", bufs=1))
        psum = ctx.enter_context(tc.psum_pool(name="psum", bufs=1))

        shared = ctx.enter_context(tc.tile_pool(name="shared", bufs=1))
        banks = [psum.tile([P, N], F32, name="bank%d" % b) for b in range(8)]

        def bank_tile(b, shape):
            if len(shape) == 2:
                return banks[b]
            return banks[b][:, : shape[1] * shape[2]].rearrange("p (a c) -> p a c", a=shape[1])

        def tenant(name, shape, dtype, room):
            return shared.tile(shape, dtype, name=name, align_bytes=64, offset=ROOMS[room])

        def quantise(name, grouped, fmt, slot="", parts=1, words=K_PASS, room=None):
            if room is None:
                codes = keep.tile([P, words], U32, name=name + "_codes", tag=slot, align_bytes=64)
            else:
                codes = tenant(name + "_codes", [P, words], U32, room)
            scales = keep.tile([P, words], U8, name=name + "_scales", align_bytes=64)
            width = words // parts
            for lo in range(0, words, width):
                nc.vector.quantize_mx(
                    out=codes[:, lo : lo + width].bitcast(fmt),
                    scales=scales[:, lo : lo + width],
                    in_=grouped[:, lo * PACK : (lo + width) * PACK],
                )
            return codes, scales, fmt

        def multiply(bank, stationary, q, moving, start, stop):
            cols = slice(q * P, (q + 1) * P)
            nc.tensor.matmul_mx(
                out=bank[:],
                lhsT=stationary[0][:, cols].bitcast(stationary[2]),
                lhsT_scale=stationary[1][:, cols],
                rhs=moving[0][:].bitcast(moving[2]),
                rhs_scale=moving[1][:],
                start=start,
                stop=stop,
            )

        def turn(grouped, u, b):
            words = grouped[:].bitcast(F32)
            bank = bank_tile(b, [P, PACK, P])
            for a in range(PACK):
                nc.tensor.transpose(bank[:, a, :], words[:, 2 * P * a + u : 2 * P * (a + 1) : 2], identity[:])
            return banks[b][:].bitcast(BF16).rearrange("s (a p e) -> s a p e", a=PACK, e=2)

        offsets = keep.tile([P, N // 16], U16, name="offsets")
        ts_row = keep.tile([P, T], F32, name="ts_row")
        nc.vector.memset(ts_row[0 : P - 1, :].bitcast(I32), 0)
        padded = keep.tile([P, ROW_PASSES, 2 * PACK], F32, name="weights")
        weights = padded[:, :, :PACK]
        nc.scalar.dma_start(weights, wt[0].rearrange("(g p t) o -> p g (t o)", p=P, t=PACK))
        nc.scalar.dma_start(ts_row[P - 1 : P, :], ts[0:1, :])
        x_view = xT[0].rearrange("(p j) r -> p j r", j=PACK)
        y_view = y[0].rearrange("(g p t) i -> g p t i", p=P, t=PACK)
        xm_view = xm[0].rearrange("(g p t) d -> g p t d", p=P, t=PACK)

        def load_x(g):
            piece = keep.tile([P, PACK, K_PASS], F32, name="x_raw%d" % g, tag="sig0" if g else "w_by_i", align_bytes=64)
            nc.sync.dma_start(piece[:], x_view[:, :, g * K_PASS : (g + 1) * K_PASS])
            return piece

        def load_y(g):
            nc.sync.dma_start(signed[g][:, 0:2, :], y_view[g][:, 0:2, :])
            late = keep.tile([P, 2, N], F32, name="late_signs%d" % g, tag="late%d" % g, align_bytes=64)
            nc.sync.dma_start(late[:], y_view[g][:, 2:PACK, :])
            return late

        def load_xm(g):
            rows = keep.tile([P, PACK, D], F32, name="xm_raw%d" % g, tag="xm_raw%d" % g)
            nc.sync.dma_start(rows[:], xm_view[g])
            return rows

        w_planes = []
        for j in range(PACK):
            plane = keep.tile([P, T], F32, name="w_plane%d" % j, tag="plane%d" % j, align_bytes=64)
            nc.sync.dma_start(plane[:], wT.rearrange("(p j) c -> p j c", j=PACK)[:, j, :])
            w_planes.append(plane)
            if j == 0:
                nc.sync.dma_start(offsets[:], offs)
        x_raw = [load_x(0)]
        signed_rows = [keep.tile([P, PACK * N], F32, name="signed%d" % g, align_bytes=64) for g in range(ROW_PASSES)]
        signed = [rows[:].rearrange("p (t i) -> p t i", t=PACK) for rows in signed_rows]
        late_signs = [load_y(0)]
        x_raw.append(load_x(1))
        late_signs.append(load_y(1))
        xm_raw = [load_xm(0), load_xm(1)]

        identity = keep.tile([P, P], F32, name="identity")
        make_identity(nc, identity[:])
        warm = keep.tile([P, 1], F32, name="warm")
        nc.scalar.activation(warm[:], padded[:, 0, 0:1], ACT.Sigmoid)
        windows = []

        def clear_window(engine, slot):
            window = keep.tile([P, T], F32, name="window%d" % len(windows), tag=slot, align_bytes=64)
            engine.memset(window[:].bitcast(I32), 0)
            windows.append(window)

        clear_window(nc.vector, "window0")
        clear_window(nc.vector, "window1")

        negated = keep.tile([P, ROW_PASSES * PACK], F32, name="negated")
        guarded = keep.tile([P, ROW_PASSES * PACK], F32, name="guarded")
        inverse = keep.tile([P, ROW_PASSES * PACK], F32, name="inverse")
        nc.vector.tensor_scalar(negated[:].rearrange("p (g t) -> p g t", t=PACK), weights, -1.0, None, ALU.mult)
        nc.vector.scalar_tensor_tensor(guarded[:].rearrange("p (g t) -> p g t", t=PACK), weights, 0.0, weights, ALU.is_equal, ALU.add)
        nc.vector.reciprocal(inverse[:], guarded[:])

        w_by_d = keep.tile([P, N * PACK], BF16, name="w_by_d", align_bytes=64)
        ts_listed = keep.tile([P, N], F32, name="ts_listed")
        for j in range(PACK):
            nc.vector.tensor_copy(
                w_by_d[:].rearrange("p (a s j) -> p s a j", a=PACK, j=PACK)[:, :, :, j], w_planes[j][:].indirect(offsets[:])
            )
        nc.scalar.activation(ts_listed[:], ts_row[:].indirect(offsets[:]), ACT.Copy)
        w_d = quantise("w_d", w_by_d, E4M3)

        ts_down = keep.tile([P, PACK], F32, name="ts_down")
        for half in range(2):
            bank = bank_tile(4 + half, [P, 2, P])
            for c in range(2):
                block = 2 * half + c
                nc.tensor.transpose(bank[:, c, :], ts_listed[:, block * P : (block + 1) * P], identity[:])
            nc.scalar.copy(ts_down[:, 2 * half : 2 * half + 2], bank[:, :, P - 1])
        ts_bank = bank_tile(7, [P, N])
        for c in range(PACK):
            nc.tensor.transpose(ts_bank[:, c * P : (c + 1) * P], ts_down[:, c : c + 1].to_broadcast([P, P]), identity[:])

        sizes = keep.tile([P, ROW_PASSES, 2, N], F32, name="sizes", tag="sizes", align_bytes=64)
        for g in range(ROW_PASSES):
            for e in range(2):
                col = g * PACK + 2 + e
                nc.scalar.activation(sizes[:, g, e, :], ts_bank[:], ACT.Copy, scale=negated[:, col : col + 1])

        def cast_x(g, shares):
            grouped = signed_rows[g][:, 2 * N :].bitcast(BF16)
            dealt = grouped.rearrange("p (t m j) -> p m j t", t=PACK, j=PACK)
            source = x_raw[g][:].rearrange("p j (m t) -> p m j t", t=PACK)
            for copy, lo, hi in shares:
                copy(dealt[:, lo:hi, :, :], source[:, lo:hi, :, :])
            return grouped

        def cast_xm_low(grouped, g):
            woven = grouped.rearrange("p (c e t) -> p c t e", e=PACK, t=PACK)
            source = xm_raw[g][:, :, : D // 2].rearrange("p t (c e) -> p c t e", e=PACK)
            nc.scalar.copy(woven, source)

        def late_xm(j):
            grouped = tenant("xm_late%d" % j, [P, ROW_PASSES * K_PASS], BF16, "xm_late%d" % j)
            for g in range(ROW_PASSES):
                woven = grouped[:, g * K_PASS : (g + 1) * K_PASS].rearrange("p (d t) -> p d t", t=PACK)
                source = xm_raw[g][:, :, j * P : (j + 1) * P].rearrange("p t d -> p d t")
                nc.gpsimd.tensor_scalar(woven, source, 1.0, 0.0, ALU.mult, ALU.add)
            return grouped

        def factor(g, places):
            for t in places:
                col = g * PACK + t
                nc.vector.scalar_tensor_tensor(
                    signed[g][:, t, :], signed[g][:, t, :], negated[:, col : col + 1], ts_bank[:], ALU.mult, ALU.mult
                )

        def factor_late(g):
            for e in range(2):
                nc.gpsimd.tensor_tensor(signed[g][:, 2 + e, :], late_signs[g][:, e, :], sizes[:, g, e, :], ALU.mult)

        def scores(g, x_d, picked):
            sig = keep.tile([P, PACK, N], F32, name="sig%d" % g, tag="sig%d" % g, align_bytes=64)
            logits = keep.tile([P, PACK, N], F32, name="logits%d" % g, tag="logits%d" % g, align_bytes=64)
            for t in range(PACK):
                col = g * PACK + t
                bank = bank_tile(picked[t], [P, N])
                multiply(bank, x_d, t, w_d, True, True)
                nc.vector.tensor_tensor(
                    logits[:, t, :].rearrange("p (s a) -> p s a", a=PACK),
                    bank[:].rearrange("p (a s) -> p s a", a=PACK),
                    signed[g][:, t, :].rearrange("p (s a) -> p s a", a=PACK),
                    ALU.mult,
                )
                nc.scalar.activation(sig[:, t, :], logits[:, t, :], ACT.Sigmoid, scale=inverse[:, col : col + 1])
            return sig

        def gradient(g, sig):
            grouped = keep.tile([P, N * PACK], BF16, name="h_by_r%d" % g, align_bytes=64)
            for lo in (0, 2):
                nc.vector.tensor_tensor(
                    grouped[:].rearrange("p (a s t) -> p s t a", a=PACK, t=PACK)[:, :, :, lo : lo + 2],
                    sig[:].rearrange("p t (s a) -> p s t a", a=PACK)[:, :, :, lo : lo + 2],
                    signed[g].rearrange("p t (s a) -> p s t a", a=PACK)[:, :, :, lo : lo + 2],
                    ALU.mult,
                )
            return grouped

        def turn_h(turned, grouped, u, b):
            view = turned.rearrange("s (e p a) -> s e p a", e=2, a=PACK)
            nc.scalar.copy(view, turn(grouped, u, b).rearrange("s a p e -> s e p a"))

        def rows_gradient(copy, result, h_i, q, w_i, b):
            bank = bank_tile(b, [P, D])
            multiply(bank, h_i, q, w_i, True, True)
            copy(result, bank[:])

        def store_rows(engine, g, lo, hi, result):
            out_view = out_1[0].rearrange("(g p t) d -> g p t d", p=P, t=PACK)[g]
            engine.dma_start(out_view[:, lo:hi, :], result)

        def unload(copy, listed, b, lo, hi):
            ordered = listed[:].rearrange("p (s a) -> p s a", a=PACK)
            copy(ordered[:, lo:hi, :], banks[b][:].rearrange("p (a s) -> p s a", a=PACK)[:, lo:hi, :])

        def table_gradient(copy, j, xm_r, q, b, slot, groups=P, step=2):
            bank = bank_tile(b, [P, N])
            multiply(bank, xm_r, q, h_r0, True, False)
            multiply(bank, xm_r, step + q, h_r1, False, True)
            listed = tenant("listed%d" % j, [P, N], F32, slot)
            unload(copy, listed, b, 0, groups)
            return listed

        def scatter_vector(j, listed, lo=0, hi=N):
            nc.vector.tensor_copy(windows[j][:].indirect(offsets[:, lo // 16 : hi // 16]), listed[:, lo:hi])

        def scatter_scalar(j, listed, half):
            part = offsets[:, half * N // 32 : (half + 1) * N // 32]
            nc.scalar.activation(windows[j][:].indirect(part), listed[:, half * N // 2 : (half + 1) * N // 2], ACT.Copy)

        def store_window(engine, j):
            engine.dma_start(out_0[j * P : (j + 1) * P, :], windows[j][:])

        x_grouped0 = cast_x(0, ((nc.vector.tensor_copy, 0, X0_VECTOR), (nc.scalar.copy, X0_VECTOR, P)))
        w_by_i = keep.tile([P, D * PACK], BF16, name="w_by_i", tag="w_by_i", align_bytes=64)
        w_view = w_by_i[:].rearrange("s (p u e a) -> s u p e a", u=2, e=2, a=PACK)
        for u in range(2):
            nc.scalar.copy(w_view[:, u, :, :, :], turn(w_by_d, u, 4 + u).rearrange("s a p e -> s p e a"))
        x_d0 = quantise("x_d0", x_grouped0, E4M3)
        factor(0, range(2))
        factor_late(0)
        x_grouped1 = cast_x(1, ((nc.scalar.copy, X1_VECTOR, P),))
        sig0 = scores(0, x_d0, (0, 1, 2, 3))
        cast_x(1, ((nc.vector.tensor_copy, 0, X1_VECTOR),))
        factor(1, range(1))
        x_d1 = quantise("x_d1", x_grouped1, E4M3)
        factor(1, range(1, 2))
        factor_late(1)
        clear_window(nc.gpsimd, "sizes")
        clear_window(nc.gpsimd, "late1")
        xm_low = keep.tile([P, D * PACK], BF16, name="xm_low", tag="logits0", align_bytes=64)
        cast_xm_low(xm_low[:, : 2 * D], 0)
        sig1 = scores(1, x_d1, (4, 5, 6, 0))
        h0 = gradient(0, sig0)
        cast_xm_low(xm_low[:, 2 * D :], 1)
        half = 2 * K_PASS
        turned0 = tenant("h_by_i0", [P, 2 * half], BF16, "turned")
        for u in range(2):
            turn_h(turned0[:, u * half : (u + 1) * half], h0, u, 1 + u)
        h1 = gradient(1, sig1)
        turned1 = [keep.tile([P, half], BF16, name="h_by_i1_0", align_bytes=64), tenant("h_by_i1_1", [P, half], BF16, "turned_last")]
        turn_h(turned1[0][:], h1, 0, 3)
        turn_h(turned1[1][:], h1, 1, 7)
        h_r0 = quantise("h_r0", h0, E5M2, slot="sig1")
        xm_r_low = quantise("xm_r_low", xm_low, E4M3)
        h_r1 = quantise("h_r1", h1, E5M2)
        listed0 = table_gradient(nc.scalar.copy, 0, xm_r_low, 0, 4, "listed_vector")
        w_i = quantise("w_i", w_by_i, E4M3, slot="logits0")
        h_i0a = quantise("h_i0a", turned0[:, :half], E5M2, words=2 * P)
        h_i0b = quantise("h_i0b", turned0[:, half:], E5M2, words=2 * P)
        h_i1a = quantise("h_i1a", turned1[0], E5M2, words=2 * P)
        h_i1b = quantise("h_i1b", turned1[1], E5M2, words=2 * P)
        scatter_vector(0, listed0)
        store_window(nc.sync, 0)
        late = [late_xm(2), late_xm(3)]
        rows1a = keep.tile([P, 2, D], F32, name="rows1a", tag="plane1", align_bytes=64)
        rows0 = keep.tile([P, PACK, D], F32, name="rows0", tag="plane0", align_bytes=64)
        for t, b in enumerate((5, 6, 0, 1)):
            rows_gradient(nc.scalar.copy, rows0[:, t, :], h_i0b if t >= 2 else h_i0a, t % 2, w_i, b)
            if t:
                store_rows(nc.scalar, 0, t - 1, t, rows0[:, t - 1 : t, :])
        rows_gradient(nc.scalar.copy, rows1a[:, 0, :], h_i1a, 0, w_i, 2)
        store_rows(nc.scalar, 0, 3, PACK, rows0[:, 3:, :])
        listed1 = table_gradient(nc.scalar.copy, 1, xm_r_low, 1, 6, "listed_scalar", P // 2)
        store_rows(nc.scalar, 1, 0, 1, rows1a[:, 0:1, :])
        unload(nc.scalar.copy, listed1, 6, P // 2, P)
        scatter_scalar(1, listed1, 0)
        rows_gradient(nc.scalar.copy, rows1a[:, 1, :], h_i1a, 1, w_i, 3)
        scatter_scalar(1, listed1, 1)
        store_rows(nc.scalar, 1, 1, 2, rows1a[:, 1:2, :])
        xm_r2 = quantise("xm_r2", late[0], E4M3, words=2 * P, room="codes2")
        xm_r3 = quantise("xm_r3", late[1], E4M3, words=2 * P, room="codes3")
        rows1b = tenant("rows1b", [P, 2, D], F32, "last_rows")
        rows_gradient(nc.vector.tensor_copy, rows1b[:, 0, :], h_i1b, 0, w_i, 7)
        rows_gradient(nc.vector.tensor_copy, rows1b[:, 1, :], h_i1b, 1, w_i, 5)
        store_rows(nc.sync, 1, 2, PACK, rows1b[:])
        listed2 = table_gradient(nc.vector.tensor_copy, 2, xm_r2, 0, 0, "listed_late", step=1)
        scatter_vector(2, listed2)
        store_window(nc.sync, 2)
        listed3 = table_gradient(nc.scalar.copy, 3, xm_r3, 0, 7, "listed_scalar", P // 2, step=1)
        store_window(nc.scalar, 1)
        unload(nc.scalar.copy, listed3, 7, P // 2, P)
        for piece in range(2):
            scatter_scalar(3, listed3, piece)
        store_window(nc.scalar, 3)
